import numpy as np
import ml_dtypes


def mxq(x, axis, fmt="e4m3"):
    dtype, down = {"e4m3": (ml_dtypes.float8_e4m3fn, 7), "e5m2": (ml_dtypes.float8_e5m2, 14)}[fmt]
    v = np.moveaxis(np.asarray(x, np.float32).astype(ml_dtypes.bfloat16).astype(np.float64), axis, -1)
    blocks = v.reshape(v.shape[:-1] + (-1, 32))
    amax = np.abs(blocks).max(-1, keepdims=True)
    byte = np.maximum(np.where(amax > 0, np.frexp(amax)[1] - 1 + 127, 0) - down, 1)
    scale = np.exp2(byte - 127.0)
    codes = (blocks / scale).astype(np.float32).astype(dtype).astype(np.float64)
    return np.moveaxis((codes * scale).reshape(v.shape), -1, axis)


WIDE = False


def mx_kscale(k):
    if not WIDE:
        return np.ones(k)
    levels = np.array([10, -10, 5, -5, 0])
    if k % 512:
        return np.exp2(np.random.permutation(np.resize(levels, k // 32))).repeat(32)
    a = np.empty((k // 512, 16))
    for p in range(k // 512):
        a[p, :8] = np.random.permutation(np.resize(levels, 8))
        for g in range(8):
            far = levels[np.abs(levels - a[p, g]) >= 10]
            a[p, g + 8] = far[np.random.randint(len(far))]
    return np.exp2(a.ravel()).repeat(32)


def f64(x):
    return np.asarray(x).astype(np.float64)


def striped(idx):
    return np.tile(np.asarray(idx).reshape(-1, 16).T, (8, 1)).astype(np.uint16)


def unstriped(offs):
    return offs[:16].T.reshape(-1).astype(np.int64)


E2M1 = np.array([0.0, 0.5, 1.0, 1.5, 2.0, 3.0, 4.0, 6.0, -0.0, -0.5, -1.0, -1.5, -2.0, -3.0, -4.0, -6.0])


def pack_weight(w, fmt):
    k, n = w.shape
    w = f64(np.asarray(w, np.float32).astype(ml_dtypes.bfloat16)).reshape(k // 32, 32, n)
    amax = np.abs(w).max(1)
    if fmt == "e4m3":
        byte = np.frexp(amax)[1] - 1 + 127 - 7
    else:
        mant, ex = np.frexp(amax / 6.0)
        byte = np.where(mant > 0.5, ex, ex - 1) + 127
    byte = np.clip(np.where(amax > 0, byte, 1), 1, 254)
    scaled = (w * np.exp2(127.0 - byte)[:, None, :]).reshape(k, n).astype(np.float32)
    by_word = np.ascontiguousarray(scaled.reshape(k // 512, 128, 4, n).transpose(0, 1, 3, 2))
    if fmt == "e4m3":
        words = by_word.astype(ml_dtypes.float8_e4m3fn).view(np.uint8)
    else:
        c = by_word.astype(ml_dtypes.float4_e2m1fn).view(np.uint8) & 0xF
        words = (c[..., 0::2] | (c[..., 1::2] << 4)).reshape(k // 512, 128, 2 * n)
    return np.ascontiguousarray(words), np.ascontiguousarray(byte.astype(np.uint8).reshape(k // 512, 16, n))


def unpack_weight(words, scales, fmt):
    g, _, n = scales.shape
    words = np.ascontiguousarray(words).reshape(g, 128, n, -1)
    if fmt == "e4m3":
        vals = words.view(ml_dtypes.float8_e4m3fn).astype(np.float64)
    else:
        nib = np.empty((g, 128, n, 4), np.uint8)
        nib[..., 0::2] = words & 0xF
        nib[..., 1::2] = words >> 4
        vals = E2M1[nib]
    vals = vals * np.repeat(np.exp2(scales.astype(np.float64) - 127.0), 8, axis=1)[..., None]
    return vals.transpose(0, 1, 3, 2).reshape(g * 512, n)


D, T, U, Q, V, I = 512, 1024, 512, 256, 2048, 512


def setup_inputs():
    n = np.random.standard_normal
    idx = np.random.permutation(T)[:Q]
    idx2 = np.random.randint(0, U, Q)
    idx3 = np.random.permutation(V)[:I]
    fd = mx_kscale(D)
    trep = pack_weight(n((D, V)) / fd[:, None], "e4m3")
    timp = pack_weight(n((D, V)) / fd[:, None], "e4m3")
    return {
        "hre": (n((D, T)) * 0.1 * fd[:, None]).astype(np.float32),
        "him": (n((D, T)) * 0.1 * fd[:, None]).astype(np.float32),
        "rre": (n((D, U)) * 0.6).astype(np.float32),
        "rim": (n((D, U)) * 0.6).astype(np.float32),
        "tre_words": trep[0],
        "tre_scales": trep[1],
        "tim_words": timp[0],
        "tim_scales": timp[1],
        "offs": striped(idx),
        "offs2": striped(idx2),
        "offs3": striped(idx3),
    }


def reference(hre, him, rre, rim, tre_words, tre_scales, tim_words, tim_scales, offs, offs2, offs3):
    idx = unstriped(offs)
    idx2 = unstriped(offs2)
    idx3 = unstriped(offs3)
    treu = unpack_weight(tre_words, tre_scales, "e4m3")
    timu = unpack_weight(tim_words, tim_scales, "e4m3")
    x = f64(hre)[:, idx] * f64(rre)[:, idx2] - f64(him)[:, idx] * f64(rim)[:, idx2]
    z = f64(hre)[:, idx] * f64(rim)[:, idx2] + f64(him)[:, idx] * f64(rre)[:, idx2]
    xq = mxq(x, 0, "e4m3")
    treidx3g = treu[:, idx3]
    zq = mxq(z, 0, "e4m3")
    timidx3g = timu[:, idx3]
    y = xq.T @ treidx3g + zq.T @ timidx3g
    return y

@@ -1,0 +1,169 @@
+from contextlib import ExitStack
+
+import concourse.mybir as mybir
+from concourse.masks import make_identity
+
+D, T, U, Q, V, I = 512, 1024, 512, 256, 2048, 512
+FLOPS = 2 * 2 * D * Q * I
+
+F32 = mybir.dt.float32
+BF16 = mybir.dt.bfloat16
+I32 = mybir.dt.int32
+U32 = mybir.dt.uint32
+U16 = mybir.dt.uint16
+U8 = mybir.dt.uint8
+FP8X4 = mybir.dt.float8_e4m3fn_x4
+MULT = mybir.AluOpType.mult
+
+P = 128
+PACK = 4
+QH = Q // P
+IH = 2
+IW = I // IH
+
+
+def tile_attend_complexscores_kernel(
+    tc, hre, him, rre, rim, tre_words, tre_scales, tim_words, tim_scales, offs, offs2, offs3, out
+):
+    nc = tc.nc
+    with ExitStack() as ctx:
+        keep = ctx.enter_context(tc.tile_pool(name="keep", bufs=1))
+        fwd_pool = ctx.enter_context(tc.psum_pool(name="fwd", bufs=2))
+        psum = ctx.enter_context(tc.psum_pool(name="psum", bufs=1))
+
+        head_list = keep.tile([P, Q // 16], U16, name="head_list")
+        rel_list = keep.tile([P, Q // 16], U16, name="rel_list")
+        tail_list = keep.tile([P, I // 16], U16, name="tail_list")
+
+        ident = keep.tile([P, P], F32, name="ident")
+        make_identity(nc, ident[:])
+
+        tail_scales = [keep.tile([P, V], U8, name="tail_scales%d" % c, align_bytes=64) for c in range(2)]
+        nc.vector.memset(tail_scales[0][:].bitcast(I32), 0)
+        nc.vector.memset(tail_scales[1][:].bitcast(I32), 0)
+        tail_words = [keep.tile([P, V], I32, name="tail_words%d" % c, align_bytes=64) for c in range(2)]
+
+        rel_tab = {}
+        head_tab = {}
+        for c in range(2):
+            for t in range(PACK):
+                rel_tab[c, t] = keep.tile([P, U], F32, name="rel_tab%d%d" % (c, t))
+                head_tab[c, t] = keep.tile([P, T], F32, name="head_tab%d%d" % (c, t), tag="head_tab%d%d" % (c, t))
+
+        rel_planes = [src.rearrange("(p t) u -> t p u", t=PACK) for src in (rre, rim)]
+        head_planes = [src.rearrange("(p t) n -> t p n", t=PACK) for src in (hre, him)]
+
+        def load_scale_rows(c, quad):
+            src = (tre_scales, tim_scales)[c]
+            nc.sync.dma_start(
+                out=tail_scales[c][32 * quad : 32 * quad + 4, :].bitcast(I32),
+                in_=src[0, 4 * quad : 4 * quad + 4, :].bitcast(I32),
+            )
+
+        nc.sync.dma_start(rel_list[:], offs2)
+        for t in range(PACK):
+            for c in range(2):
+                nc.sync.dma_start(out=rel_tab[c, t][:], in_=rel_planes[c][t])
+            if t == 0:
+                nc.sync.dma_start(head_list[:], offs)
+            for c in range(2):
+                nc.sync.dma_start(out=head_tab[c, t][:], in_=head_planes[c][t])
+                load_scale_rows(c, t)
+        nc.sync.dma_start(tail_list[:], offs3)
+        for c, src in enumerate((tre_words, tim_words)):
+            nc.sync.dma_start(out=tail_words[c][:], in_=src[0].rearrange("p n t -> p (n t)").bitcast(I32))
+
+        back = [psum.tile([P, 2, 2, P], F32, name="back%d" % h) for h in range(QH)]
+        for u in range(2):
+            fwd = [fwd_pool.tile([P, 2, 2, P], F32, name="fwd") for h in range(QH)]
+            for e in range(2):
+                t = 2 * u + e
+                rel = keep.tile([P, 3, Q], F32, name="rel%d" % t)
+                nc.vector.tensor_copy(rel[:, 1, :], rel_tab[0, t][:].indirect(rel_list[:]))
+                nc.vector.tensor_copy(rel[:, 2, :], rel_tab[1, t][:].indirect(rel_list[:]))
+                nc.scalar.mul(rel[:, 0, :], rel[:, 2, :], -1.0)
+                prods = []
+                for c in range(2):
+                    head = keep.tile([P, 1, Q], F32, name="head%d%d" % (c, t), tag="head%d%d" % (c, t), align_bytes=64)
+                    nc.vector.tensor_copy(head[:, 0, :], head_tab[c, t][:].indirect(head_list[:]))
+                    prods.append(head)
+                for c in range(2):
+                    prod = keep.tile([P, 2, Q], F32, name="prod%d%d" % (c, t), tag=("head_tab1%d" % t if c == 0 else "prod%d" % t))
+                    nc.vector.tensor_tensor(
+                        prod[:], prods[c][:].to_broadcast([P, 2, Q]), rel[:, 1 - c : 3 - c, :], MULT
+                    )
+                    prods[c] = prod
+                for h in range(QH):
+                    for w in range(2):
+                        for c in range(2):
+                            nc.tensor.matmul(
+                                fwd[h][:, w, e, :],
+                                prods[c][:, w, h * P : (h + 1) * P],
+                                ident[:],
+                                start=(c == 0),
+                                stop=(c == 1),
+                                is_transpose=True,
+                            )
+            for h in range(QH):
+                turned = keep.tile([P, 2, P, 2], BF16, name="turned%d%d" % (u, h))
+                nc.scalar.copy(turned[:], fwd[h][:].rearrange("q w e p -> q w p e"))
+                turned_words = turned[:].rearrange("q w p e -> q (w p e)").bitcast(F32)
+                for w in range(2):
+                    nc.tensor.transpose(back[h][:, w, u, :], turned_words[:, w * P : (w + 1) * P], ident[:])
+
+        picked_scales = []
+        picked_words = []
+        for c in range(2):
+            ps = keep.tile([P, I], U8, name="picked_scales%d" % c, tag="head%d3" % c, align_bytes=64)
+            nc.vector.tensor_copy(ps[:], tail_scales[c][:].indirect(tail_list[:]))
+            picked_scales.append(ps)
+            pw = keep.tile([P, I], U32, name="picked_words%d" % c, align_bytes=64)
+            picked_words.append(pw)
+        nc.vector.tensor_copy(picked_words[0][:], tail_words[0][:].bitcast(U32).indirect(tail_list[:]))
+
+        codes = []
+        scales = []
+        for h in range(QH):
+            grouped = keep.tile([P, 2 * P * PACK], BF16, name="grouped%d" % h, align_bytes=64)
+            nc.scalar.copy(
+                grouped[:].bitcast(F32).rearrange("p (w q u) -> p w q u", w=2, u=2),
+                back[h][:].rearrange("p w u q -> p w q u"),
+            )
+            cd = keep.tile([P, 2 * P], U32, name="codes%d" % h, align_bytes=64)
+            sc = keep.tile([P, 2 * P], U8, name="scales%d" % h, align_bytes=64)
+            nc.vector.quantize_mx(out=cd[:].bitcast(FP8X4), scales=sc[:], in_=grouped[:])
+            codes.append(cd)
+            scales.append(sc)
+
+        def mx_pass(acc, h, w, cols):
+            nc.tensor.matmul_mx(
+                out=acc[:],
+                lhsT=codes[h][:, w * P : (w + 1) * P].bitcast(FP8X4),
+                lhsT_scale=scales[h][:, w * P : (w + 1) * P],
+                rhs=picked_words[w][:, cols].bitcast(FP8X4),
+                rhs_scale=picked_scales[w][:, cols],
+                start=(w == 0),
+                stop=(w == 1),
+            )
+
+        accs = {}
+        for j in range(IH):
+            for h in range(QH):
+                accs[j, h] = psum.tile([P, IW], F32, name="acc%d%d" % (j, h))
+                mx_pass(accs[j, h], h, 0, slice(j * IW, (j + 1) * IW))
+        for j in range(IH):
+            cols = slice(j * IW, (j + 1) * IW)
+            nc.vector.tensor_copy(
+                picked_words[1][:, cols],
+                tail_words[1][:].bitcast(U32).indirect(tail_list[:, j * IW // 16 : (j + 1) * IW // 16]),
+            )
+        for j in range(IH):
+            cols = slice(j * IW, (j + 1) * IW)
+            for h in range(QH):
+                mx_pass(accs[j, h], h, 1, cols)
+                result = keep.tile([P, IW], F32, name="result%d%d" % (j, h))
+                if j == IH - 1 and h == QH - 1:
+                    nc.vector.tensor_copy(result[:], accs[j, h][:])
+                else:
+                    nc.scalar.copy(result[:], accs[j, h][:])
+                nc.sync.dma_start(out=out[h * P : (h + 1) * P, cols], in_=result[:])

@@ -48,7 +48,7 @@ def tile_attend_complexscores_kernel(
         for c in range(2):
             for t in range(PACK):
                 rel_tab[c, t] = keep.tile([P, U], F32, name="rel_tab%d%d" % (c, t))
-                head_tab[c, t] = keep.tile([P, T], F32, name="head_tab%d%d" % (c, t), tag="head_tab%d%d" % (c, t))
+                head_tab[c, t] = keep.tile([P, T], F32, name="head_tab%d%d" % (c, t))
 
         rel_planes = [src.rearrange("(p t) u -> t p u", t=PACK) for src in (rre, rim)]
         head_planes = [src.rearrange("(p t) n -> t p n", t=PACK) for src in (hre, him)]
@@ -68,12 +68,14 @@ def tile_attend_complexscores_kernel(
                 nc.sync.dma_start(head_list[:], offs)
             for c in range(2):
                 nc.sync.dma_start(out=head_tab[c, t][:], in_=head_planes[c][t])
-                load_scale_rows(c, t)
-        nc.sync.dma_start(tail_list[:], offs3)
+                load_scale_rows(t // 2, 2 * (t % 2) + c)
+            if t == 0:
+                nc.sync.dma_start(tail_list[:], offs3)
         for c, src in enumerate((tre_words, tim_words)):
             nc.sync.dma_start(out=tail_words[c][:], in_=src[0].rearrange("p n t -> p (n t)").bitcast(I32))
 
         back = [psum.tile([P, 2, 2, P], F32, name="back%d" % h) for h in range(QH)]
+        picked_scales = []
         for u in range(2):
             fwd = [fwd_pool.tile([P, 2, 2, P], F32, name="fwd") for h in range(QH)]
             for e in range(2):
@@ -84,12 +86,13 @@ def tile_attend_complexscores_kernel(
                 nc.scalar.mul(rel[:, 0, :], rel[:, 2, :], -1.0)
                 prods = []
                 for c in range(2):
-                    head = keep.tile([P, 1, Q], F32, name="head%d%d" % (c, t), tag="head%d%d" % (c, t), align_bytes=64)
+                    head = keep.tile([P, 1, Q], F32, name="head%d%d" % (c, t))
                     nc.vector.tensor_copy(head[:, 0, :], head_tab[c, t][:].indirect(head_list[:]))
                     prods.append(head)
                 for c in range(2):
-                    prod = keep.tile([P, 2, Q], F32, name="prod%d%d" % (c, t), tag=("head_tab1%d" % t if c == 0 else "prod%d" % t))
-                    nc.vector.tensor_tensor(
+                    prod = keep.tile([P, 2, Q], F32, name="prod%d%d" % (c, t))
+                    engine = nc.vector if (t, c) == (PACK - 1, 1) else nc.gpsimd
+                    engine.tensor_tensor(
                         prod[:], prods[c][:].to_broadcast([P, 2, Q]), rel[:, 1 - c : 3 - c, :], MULT
                     )
                     prods[c] = prod
@@ -104,6 +107,9 @@ def tile_attend_complexscores_kernel(
                                 stop=(c == 1),
                                 is_transpose=True,
                             )
+            ps = keep.tile([P, I], U8, name="picked_scales%d" % u, align_bytes=64)
+            nc.vector.tensor_copy(ps[:], tail_scales[u][:].indirect(tail_list[:]))
+            picked_scales.append(ps)
             for h in range(QH):
                 turned = keep.tile([P, 2, P, 2], BF16, name="turned%d%d" % (u, h))
                 nc.scalar.copy(turned[:], fwd[h][:].rearrange("q w e p -> q w p e"))
@@ -111,12 +117,8 @@ def tile_attend_complexscores_kernel(
                 for w in range(2):
                     nc.tensor.transpose(back[h][:, w, u, :], turned_words[:, w * P : (w + 1) * P], ident[:])
 
-        picked_scales = []
         picked_words = []
         for c in range(2):
-            ps = keep.tile([P, I], U8, name="picked_scales%d" % c, tag="head%d3" % c, align_bytes=64)
-            nc.vector.tensor_copy(ps[:], tail_scales[c][:].indirect(tail_list[:]))
-            picked_scales.append(ps)
             pw = keep.tile([P, I], U32, name="picked_words%d" % c, align_bytes=64)
             picked_words.append(pw)
         nc.vector.tensor_copy(picked_words[0][:], tail_words[0][:].bitcast(U32).indirect(tail_list[:]))

@@ -20,6 +20,7 @@ PACK = 4
 QH = Q // P
 IH = 2
 IW = I // IH
+ROWS = D // 32
 
 
 def tile_attend_complexscores_kernel(
@@ -28,100 +29,117 @@ def tile_attend_complexscores_kernel(
     nc = tc.nc
     with ExitStack() as ctx:
         keep = ctx.enter_context(tc.tile_pool(name="keep", bufs=1))
-        fwd_pool = ctx.enter_context(tc.psum_pool(name="fwd", bufs=2))
         psum = ctx.enter_context(tc.psum_pool(name="psum", bufs=1))
 
         head_list = keep.tile([P, Q // 16], U16, name="head_list")
         rel_list = keep.tile([P, Q // 16], U16, name="rel_list")
         tail_list = keep.tile([P, I // 16], U16, name="tail_list")
 
+        scale_tab = [keep.tile([P, V], U8, name="scale_tab%d" % c) for c in range(2)]
+        tail_scales = keep.tile([P, 2 * I], U8, name="tail_scales", align_bytes=64)
+        nc.gpsimd.memset(scale_tab[0][:].bitcast(I32), 0)
+        nc.vector.memset(scale_tab[1][:].bitcast(I32), 0)
+        nc.vector.memset(tail_scales[:].bitcast(I32), 0)
         ident = keep.tile([P, P], F32, name="ident")
         make_identity(nc, ident[:])
+        word_tab = [keep.tile([P, V], I32, name="word_tab%d" % c) for c in range(2)]
 
-        tail_scales = [keep.tile([P, V], U8, name="tail_scales%d" % c, align_bytes=64) for c in range(2)]
-        nc.vector.memset(tail_scales[0][:].bitcast(I32), 0)
-        nc.vector.memset(tail_scales[1][:].bitcast(I32), 0)
-        tail_words = [keep.tile([P, V], I32, name="tail_words%d" % c, align_bytes=64) for c in range(2)]
-
+        rel_src = [src.rearrange("(p t) u -> p t u", t=PACK) for src in (rre, rim)]
+        head_src = [src.rearrange("(p t) n -> p t n", t=PACK) for src in (hre, him)]
         rel_tab = {}
         head_tab = {}
-        for c in range(2):
-            for t in range(PACK):
-                rel_tab[c, t] = keep.tile([P, U], F32, name="rel_tab%d%d" % (c, t))
-                head_tab[c, t] = keep.tile([P, T], F32, name="head_tab%d%d" % (c, t))
 
-        rel_planes = [src.rearrange("(p t) u -> t p u", t=PACK) for src in (rre, rim)]
-        head_planes = [src.rearrange("(p t) n -> t p n", t=PACK) for src in (hre, him)]
+        def load_rel(c, t):
+            tab = keep.tile([P, U], F32, name="rel_tab%d%d" % (c, t))
+            nc.sync.dma_start(out=tab[:], in_=rel_src[c][:, t, :])
+            rel_tab[c, t] = tab[:]
 
-        def load_scale_rows(c, quad):
+        def load_head(c, t):
+            head_tab[c, t] = keep.tile([P, T], F32, name="head_tab%d%d" % (c, t))
+            nc.sync.dma_start(out=head_tab[c, t][:], in_=head_src[c][:, t, :])
+
+        def load_scales(c):
             src = (tre_scales, tim_scales)[c]
-            nc.sync.dma_start(
-                out=tail_scales[c][32 * quad : 32 * quad + 4, :].bitcast(I32),
-                in_=src[0, 4 * quad : 4 * quad + 4, :].bitcast(I32),
-            )
+            nc.sync.dma_start(out=scale_tab[c][0:ROWS, :].bitcast(I32), in_=src[0].bitcast(I32))
+
+        picked_scales = keep.tile([P, 2 * I], U8, name="picked_scales")
+
+        def pick_scales(c):
+            nc.vector.tensor_copy(picked_scales[:, c * I : (c + 1) * I], scale_tab[c][:].indirect(tail_list[:]))
 
         nc.sync.dma_start(rel_list[:], offs2)
         for t in range(PACK):
-            for c in range(2):
-                nc.sync.dma_start(out=rel_tab[c, t][:], in_=rel_planes[c][t])
+            if t == 2:
+                load_scales(1)
+            load_rel(0, t)
+            if t == 0:
+                nc.sync.dma_start(tail_list[:], offs3)
+                load_scales(0)
+            load_rel(1, t)
             if t == 0:
                 nc.sync.dma_start(head_list[:], offs)
             for c in range(2):
-                nc.sync.dma_start(out=head_tab[c, t][:], in_=head_planes[c][t])
-                load_scale_rows(t // 2, 2 * (t % 2) + c)
-            if t == 0:
-                nc.sync.dma_start(tail_list[:], offs3)
+                load_head(c, t)
         for c, src in enumerate((tre_words, tim_words)):
-            nc.sync.dma_start(out=tail_words[c][:], in_=src[0].rearrange("p n t -> p (n t)").bitcast(I32))
+            nc.sync.dma_start(out=word_tab[c][:], in_=src[0].rearrange("p n t -> p (n t)").bitcast(I32))
+
+        pick_scales(0)
+        pick_scales(1)
+        for j in range(4):
+            nc.sync.dma_start(
+                out=tail_scales[j:P:32, :].bitcast(I32), in_=picked_scales[j:ROWS:4, :].bitcast(I32)
+            )
 
         back = [psum.tile([P, 2, 2, P], F32, name="back%d" % h) for h in range(QH)]
-        picked_scales = []
         for u in range(2):
-            fwd = [fwd_pool.tile([P, 2, 2, P], F32, name="fwd") for h in range(QH)]
+            fwd = {}
+            for h in range(QH):
+                for w in range(2):
+                    fwd[h, w] = psum.tile([P, 2, P], F32, name="fwd%d%d%d" % (u, h, w), tag="bank%d%d" % (h, w))
             for e in range(2):
                 t = 2 * u + e
                 rel = keep.tile([P, 3, Q], F32, name="rel%d" % t)
-                nc.vector.tensor_copy(rel[:, 1, :], rel_tab[0, t][:].indirect(rel_list[:]))
-                nc.vector.tensor_copy(rel[:, 2, :], rel_tab[1, t][:].indirect(rel_list[:]))
+                nc.vector.tensor_copy(rel[:, 1, :], rel_tab[0, t].indirect(rel_list[:]))
+                nc.vector.tensor_copy(rel[:, 2, :], rel_tab[1, t].indirect(rel_list[:]))
                 nc.scalar.mul(rel[:, 0, :], rel[:, 2, :], -1.0)
-                prods = []
                 for c in range(2):
+                    pieces = QH if (t, c) == (PACK - 1, 1) else 1
+                    width = Q // pieces
                     head = keep.tile([P, 1, Q], F32, name="head%d%d" % (c, t))
-                    nc.vector.tensor_copy(head[:, 0, :], head_tab[c, t][:].indirect(head_list[:]))
-                    prods.append(head)
-                for c in range(2):
                     prod = keep.tile([P, 2, Q], F32, name="prod%d%d" % (c, t))
-                    engine = nc.vector if (t, c) == (PACK - 1, 1) else nc.gpsimd
-                    engine.tensor_tensor(
-                        prod[:], prods[c][:].to_broadcast([P, 2, Q]), rel[:, 1 - c : 3 - c, :], MULT
-                    )
-                    prods[c] = prod
-                for h in range(QH):
-                    for w in range(2):
-                        for c in range(2):
+                    for k in range(pieces):
+                        nc.vector.tensor_copy(
+                            head[:, 0, k * width : (k + 1) * width],
+                            head_tab[c, t][:].indirect(head_list[:, k * width // 16 : (k + 1) * width // 16]),
+                        )
+                    engine = nc.vector if t == PACK - 1 else nc.gpsimd
+                    for k in range(pieces):
+                        cols = slice(k * width, (k + 1) * width)
+                        engine.tensor_tensor(
+                            prod[:, :, cols],
+                            head[:, :, cols].to_broadcast([P, 2, width]),
+                            rel[:, 1 - c : 3 - c, cols],
+                            MULT,
+                        )
+                    for h in range(QH):
+                        for w in range(2):
                             nc.tensor.matmul(
-                                fwd[h][:, w, e, :],
-                                prods[c][:, w, h * P : (h + 1) * P],
+                                fwd[h, w][:, e, :],
+                                prod[:, w, h * P : (h + 1) * P],
                                 ident[:],
                                 start=(c == 0),
                                 stop=(c == 1),
                                 is_transpose=True,
                             )
-            ps = keep.tile([P, I], U8, name="picked_scales%d" % u, align_bytes=64)
-            nc.vector.tensor_copy(ps[:], tail_scales[u][:].indirect(tail_list[:]))
-            picked_scales.append(ps)
             for h in range(QH):
-                turned = keep.tile([P, 2, P, 2], BF16, name="turned%d%d" % (u, h))
-                nc.scalar.copy(turned[:], fwd[h][:].rearrange("q w e p -> q w p e"))
-                turned_words = turned[:].rearrange("q w p e -> q (w p e)").bitcast(F32)
                 for w in range(2):
-                    nc.tensor.transpose(back[h][:, w, u, :], turned_words[:, w * P : (w + 1) * P], ident[:])
+                    turned = keep.tile([P, P, 2], BF16, name="turned%d%d%d" % (u, h, w))
+                    nc.scalar.copy(turned[:], fwd[h, w][:].rearrange("q e p -> q p e"))
+                    turned_words = turned[:].rearrange("q p e -> q (p e)").bitcast(F32)
+                    nc.tensor.transpose(back[h][:, w, u, :], turned_words, ident[:])
 
-        picked_words = []
-        for c in range(2):
-            pw = keep.tile([P, I], U32, name="picked_words%d" % c, align_bytes=64)
-            picked_words.append(pw)
-        nc.vector.tensor_copy(picked_words[0][:], tail_words[0][:].bitcast(U32).indirect(tail_list[:]))
+        picked_words = [keep.tile([P, I], U32, name="picked_words%d" % c, align_bytes=64) for c in range(2)]
+        nc.vector.tensor_copy(picked_words[0][:], word_tab[0][:].bitcast(U32).indirect(tail_list[:]))
 
         codes = []
         scales = []
@@ -143,21 +161,21 @@ def tile_attend_complexscores_kernel(
                 lhsT=codes[h][:, w * P : (w + 1) * P].bitcast(FP8X4),
                 lhsT_scale=scales[h][:, w * P : (w + 1) * P],
                 rhs=picked_words[w][:, cols].bitcast(FP8X4),
-                rhs_scale=picked_scales[w][:, cols],
+                rhs_scale=tail_scales[:, w * I + cols.start : w * I + cols.stop],
                 start=(w == 0),
                 stop=(w == 1),
             )
 
         accs = {}
-        for j in range(IH):
-            for h in range(QH):
-                accs[j, h] = psum.tile([P, IW], F32, name="acc%d%d" % (j, h))
+        for h in range(QH):
+            for j in range(IH):
+                accs[j, h] = psum.tile([P, IW], F32, name="acc%d%d" % (j, h), tag="bank%d%d" % (h, j))
                 mx_pass(accs[j, h], h, 0, slice(j * IW, (j + 1) * IW))
         for j in range(IH):
             cols = slice(j * IW, (j + 1) * IW)
             nc.vector.tensor_copy(
                 picked_words[1][:, cols],
-                tail_words[1][:].bitcast(U32).indirect(tail_list[:, j * IW // 16 : (j + 1) * IW // 16]),
+                word_tab[1][:].bitcast(U32).indirect(tail_list[:, j * IW // 16 : (j + 1) * IW // 16]),
             )
         for j in range(IH):
             cols = slice(j * IW, (j + 1) * IW)

@@ -42,7 +42,9 @@ def tile_attend_complexscores_kernel(
         nc.vector.memset(tail_scales[:].bitcast(I32), 0)
         ident = keep.tile([P, P], F32, name="ident")
         make_identity(nc, ident[:])
-        word_tab = [keep.tile([P, V], I32, name="word_tab%d" % c) for c in range(2)]
+        word_tab = [
+            keep.tile([P, V], I32, name="word_tab%d" % c, tag="word_tab%d" % c, align_bytes=64) for c in range(2)
+        ]
 
         rel_src = [src.rearrange("(p t) u -> p t u", t=PACK) for src in (rre, rim)]
         head_src = [src.rearrange("(p t) n -> p t n", t=PACK) for src in (hre, him)]
@@ -60,35 +62,47 @@ def tile_attend_complexscores_kernel(
 
         def load_scales(c):
             src = (tre_scales, tim_scales)[c]
-            nc.sync.dma_start(out=scale_tab[c][0:ROWS, :].bitcast(I32), in_=src[0].bitcast(I32))
+            nc.sync.dma_start(out=scale_tab[c][0:P:8, :].bitcast(I32), in_=src[0].bitcast(I32))
 
         picked_scales = keep.tile([P, 2 * I], U8, name="picked_scales")
 
         def pick_scales(c):
             nc.vector.tensor_copy(picked_scales[:, c * I : (c + 1) * I], scale_tab[c][:].indirect(tail_list[:]))
 
-        nc.sync.dma_start(rel_list[:], offs2)
-        for t in range(PACK):
-            if t == 2:
-                load_scales(1)
-            load_rel(0, t)
-            if t == 0:
-                nc.sync.dma_start(tail_list[:], offs3)
-                load_scales(0)
-            load_rel(1, t)
-            if t == 0:
-                nc.sync.dma_start(head_list[:], offs)
-            for c in range(2):
-                load_head(c, t)
-        for c, src in enumerate((tre_words, tim_words)):
+        def place_scales(j):
+            nc.sync.dma_start(
+                out=tail_scales[j:P:32, :].bitcast(I32), in_=picked_scales[8 * j : P : 32, :].bitcast(I32)
+            )
+
+        def load_words(c):
+            src = (tre_words, tim_words)[c]
             nc.sync.dma_start(out=word_tab[c][:], in_=src[0].rearrange("p n t -> p (n t)").bitcast(I32))
 
+        load_rel(0, 0)
+        nc.sync.dma_start(rel_list[:], offs2)
+        load_rel(1, 0)
+        load_head(0, 0)
+        nc.sync.dma_start(head_list[:], offs)
+        nc.sync.dma_start(tail_list[:], offs3)
+        load_scales(0)
+        load_head(1, 0)
+        for t in range(1, PACK):
+            if t == 2:
+                load_scales(1)
+            for c in range(2):
+                load_rel(c, t)
+            for c in range(2):
+                if (t, c) != (PACK - 1, 1):
+                    load_head(c, t)
         pick_scales(0)
         pick_scales(1)
-        for j in range(4):
-            nc.sync.dma_start(
-                out=tail_scales[j:P:32, :].bitcast(I32), in_=picked_scales[j:ROWS:4, :].bitcast(I32)
-            )
+        place_scales(0)
+        load_head(1, PACK - 1)
+        place_scales(1)
+        load_words(0)
+        place_scales(2)
+        place_scales(3)
+        load_words(1)
 
         back = [psum.tile([P, 2, 2, P], F32, name="back%d" % h) for h in range(QH)]
         for u in range(2):
@@ -134,13 +148,15 @@ def tile_attend_complexscores_kernel(
             for h in range(QH):
                 for w in range(2):
                     turned = keep.tile([P, P, 2], BF16, name="turned%d%d%d" % (u, h, w))
-                    nc.scalar.copy(turned[:], fwd[h, w][:].rearrange("q e p -> q p e"))
+                    copy = nc.vector.tensor_copy if (u, h, w) == (1, 1, 0) else nc.scalar.copy
+                    copy(turned[:], fwd[h, w][:].rearrange("q e p -> q p e"))
                     turned_words = turned[:].rearrange("q p e -> q (p e)").bitcast(F32)
                     nc.tensor.transpose(back[h][:, w, u, :], turned_words, ident[:])
 
         picked_words = [keep.tile([P, I], U32, name="picked_words%d" % c, align_bytes=64) for c in range(2)]
         nc.vector.tensor_copy(picked_words[0][:], word_tab[0][:].bitcast(U32).indirect(tail_list[:]))
 
+        all_codes = keep.tile([P, QH * 2 * P], U32, name="codes", tag="word_tab0", align_bytes=64)
         codes = []
         scales = []
         for h in range(QH):
@@ -149,9 +165,9 @@ def tile_attend_complexscores_kernel(
                 grouped[:].bitcast(F32).rearrange("p (w q u) -> p w q u", w=2, u=2),
                 back[h][:].rearrange("p w u q -> p w q u"),
             )
-            cd = keep.tile([P, 2 * P], U32, name="codes%d" % h, align_bytes=64)
+            cd = all_codes[:, h * 2 * P : (h + 1) * 2 * P]
             sc = keep.tile([P, 2 * P], U8, name="scales%d" % h, align_bytes=64)
-            nc.vector.quantize_mx(out=cd[:].bitcast(FP8X4), scales=sc[:], in_=grouped[:])
+            nc.vector.quantize_mx(out=cd.bitcast(FP8X4), scales=sc[:], in_=grouped[:])
             codes.append(cd)
             scales.append(sc)
 

@@ -14,6 +14,7 @@ U16 = mybir.dt.uint16
 U8 = mybir.dt.uint8
 FP8X4 = mybir.dt.float8_e4m3fn_x4
 MULT = mybir.AluOpType.mult
+SUB = mybir.AluOpType.subtract
 
 P = 128
 PACK = 4
@@ -46,19 +47,22 @@ def tile_attend_complexscores_kernel(
             keep.tile([P, V], I32, name="word_tab%d" % c, tag="word_tab%d" % c, align_bytes=64) for c in range(2)
         ]
 
-        rel_src = [src.rearrange("(p t) u -> p t u", t=PACK) for src in (rre, rim)]
-        head_src = [src.rearrange("(p t) n -> p t n", t=PACK) for src in (hre, him)]
+        rel_src = [src.rearrange("(p t) u -> p (t u)", t=PACK) for src in (rre, rim)]
+        head_src = [src.rearrange("(p t) n -> p (t n)", t=PACK) for src in (hre, him)]
         rel_tab = {}
         head_tab = {}
 
-        def load_rel(c, t):
-            tab = keep.tile([P, U], F32, name="rel_tab%d%d" % (c, t))
-            nc.sync.dma_start(out=tab[:], in_=rel_src[c][:, t, :])
-            rel_tab[c, t] = tab[:]
+        def load_rel(c, t, n):
+            tab = keep.tile([P, n * U], F32, name="rel_tab%d%d" % (c, t))
+            nc.sync.dma_start(out=tab[:], in_=rel_src[c][:, t * U : (t + n) * U])
+            for e in range(n):
+                rel_tab[c, t + e] = tab[:, e * U : (e + 1) * U]
 
-        def load_head(c, t):
-            head_tab[c, t] = keep.tile([P, T], F32, name="head_tab%d%d" % (c, t))
-            nc.sync.dma_start(out=head_tab[c, t][:], in_=head_src[c][:, t, :])
+        def load_head(c, t, n):
+            tab = keep.tile([P, n * T], F32, name="head_tab%d%d" % (c, t))
+            nc.sync.dma_start(out=tab[:], in_=head_src[c][:, t * T : (t + n) * T])
+            for e in range(n):
+                head_tab[c, t + e] = tab[:, e * T : (e + 1) * T]
 
         def load_scales(c):
             src = (tre_scales, tim_scales)[c]
@@ -78,67 +82,47 @@ def tile_attend_complexscores_kernel(
             src = (tre_words, tim_words)[c]
             nc.sync.dma_start(out=word_tab[c][:], in_=src[0].rearrange("p n t -> p (n t)").bitcast(I32))
 
-        load_rel(0, 0)
-        nc.sync.dma_start(rel_list[:], offs2)
-        load_rel(1, 0)
-        load_head(0, 0)
-        nc.sync.dma_start(head_list[:], offs)
-        nc.sync.dma_start(tail_list[:], offs3)
-        load_scales(0)
-        load_head(1, 0)
-        for t in range(1, PACK):
-            if t == 2:
-                load_scales(1)
-            for c in range(2):
-                load_rel(c, t)
-            for c in range(2):
-                if (t, c) != (PACK - 1, 1):
-                    load_head(c, t)
-        pick_scales(0)
-        pick_scales(1)
-        place_scales(0)
-        load_head(1, PACK - 1)
-        place_scales(1)
-        load_words(0)
-        place_scales(2)
-        place_scales(3)
-        load_words(1)
+        x_words = keep.tile([P, 2, Q], F32, name="x_words")
+        x_back = psum.tile([P, Q], F32, name="x_back")
+        z_back = psum.tile([P, 2, Q], F32, name="z_back")
+        halves = [slice(h * P, (h + 1) * P) for h in range(QH)]
 
-        back = [psum.tile([P, 2, 2, P], F32, name="back%d" % h) for h in range(QH)]
-        for u in range(2):
+        def turn_back(name, summed, back):
+            turned = keep.tile([P, P, 2], BF16, name=name)
+            nc.scalar.copy(turned[:], summed.rearrange("q e p -> q p e"))
+            nc.tensor.transpose(back, turned[:].rearrange("q p e -> q (p e)").bitcast(F32), ident[:])
+
+        def gather_rel(t, rel):
+            for c in range(2):
+                nc.vector.tensor_copy(rel[:, c, :], rel_tab[c, t].indirect(rel_list[:]))
+
+        def gather_head(c, t, pieces):
+            head = keep.tile([P, 1, Q], F32, name="head%d%d" % (c, t))
+            width = Q // pieces
+            for k in range(pieces):
+                nc.vector.tensor_copy(
+                    head[:, 0, k * width : (k + 1) * width],
+                    head_tab[c, t].indirect(head_list[:, k * width // 16 : (k + 1) * width // 16]),
+                )
+            return head
+
+        def first_pair():
             fwd = {}
             for h in range(QH):
                 for w in range(2):
-                    fwd[h, w] = psum.tile([P, 2, P], F32, name="fwd%d%d%d" % (u, h, w), tag="bank%d%d" % (h, w))
-            for e in range(2):
-                t = 2 * u + e
+                    fwd[h, w] = psum.tile([P, 2, P], F32, name="fwd%d%d" % (h, w), tag="bank%d%d" % (h, w))
+            for t in range(2):
                 rel = keep.tile([P, 3, Q], F32, name="rel%d" % t)
-                nc.vector.tensor_copy(rel[:, 1, :], rel_tab[0, t].indirect(rel_list[:]))
-                nc.vector.tensor_copy(rel[:, 2, :], rel_tab[1, t].indirect(rel_list[:]))
+                gather_rel(t, rel[:, 1:3, :])
                 nc.scalar.mul(rel[:, 0, :], rel[:, 2, :], -1.0)
                 for c in range(2):
-                    pieces = QH if (t, c) == (PACK - 1, 1) else 1
-                    width = Q // pieces
-                    head = keep.tile([P, 1, Q], F32, name="head%d%d" % (c, t))
+                    head = gather_head(c, t, 1)
                     prod = keep.tile([P, 2, Q], F32, name="prod%d%d" % (c, t))
-                    for k in range(pieces):
-                        nc.vector.tensor_copy(
-                            head[:, 0, k * width : (k + 1) * width],
-                            head_tab[c, t][:].indirect(head_list[:, k * width // 16 : (k + 1) * width // 16]),
-                        )
-                    engine = nc.vector if t == PACK - 1 else nc.gpsimd
-                    for k in range(pieces):
-                        cols = slice(k * width, (k + 1) * width)
-                        engine.tensor_tensor(
-                            prod[:, :, cols],
-                            head[:, :, cols].to_broadcast([P, 2, width]),
-                            rel[:, 1 - c : 3 - c, cols],
-                            MULT,
-                        )
+                    nc.gpsimd.tensor_tensor(prod[:], head[:].to_broadcast([P, 2, Q]), rel[:, 1 - c : 3 - c, :], MULT)
                     for h in range(QH):
                         for w in range(2):
                             nc.tensor.matmul(
-                                fwd[h, w][:, e, :],
+                                fwd[h, w][:, t, :],
                                 prod[:, w, h * P : (h + 1) * P],
                                 ident[:],
                                 start=(c == 0),
@@ -146,38 +130,100 @@ def tile_attend_complexscores_kernel(
                                 is_transpose=True,
                             )
             for h in range(QH):
-                for w in range(2):
-                    turned = keep.tile([P, P, 2], BF16, name="turned%d%d%d" % (u, h, w))
-                    copy = nc.vector.tensor_copy if (u, h, w) == (1, 1, 0) else nc.scalar.copy
-                    copy(turned[:], fwd[h, w][:].rearrange("q e p -> q p e"))
-                    turned_words = turned[:].rearrange("q p e -> q (p e)").bitcast(F32)
-                    nc.tensor.transpose(back[h][:, w, u, :], turned_words, ident[:])
+                turn_back("x_turned%d" % h, fwd[h, 0][:], x_back[:, halves[h]])
+            nc.scalar.copy(x_words[:, 0, :], x_back[:])
+            for h in range(QH):
+                turn_back("z_turned0%d" % h, fwd[h, 1][:], z_back[:, 0, halves[h]])
 
-        picked_words = [keep.tile([P, I], U32, name="picked_words%d" % c, align_bytes=64) for c in range(2)]
-        nc.vector.tensor_copy(picked_words[0][:], word_tab[0][:].bitcast(U32).indirect(tail_list[:]))
+        def second_pair():
+            fwd = [psum.tile([P, 2, P], F32, name="z_fwd%d" % h) for h in range(QH)]
+            prod = [keep.tile([P, 2, 2, Q], F32, name="prod%d" % c) for c in range(2)]
+            for e in range(2):
+                t = 2 + e
+                rel = keep.tile([P, 2, Q], F32, name="rel%d" % t)
+                gather_rel(t, rel[:])
+                for c in range(2):
+                    last = (e, c) == (1, 1)
+                    head = gather_head(c, t, QH if last else 1)
+                    engine = nc.vector if e == 1 else nc.gpsimd
+                    for cols in halves if last else [slice(0, Q)]:
+                        engine.tensor_tensor(
+                            prod[c][:, e, :, cols],
+                            head[:, :, cols].to_broadcast([P, 2, cols.stop - cols.start]),
+                            rel[:, :, cols],
+                            MULT,
+                        )
+                    for h in range(QH):
+                        nc.tensor.matmul(
+                            fwd[h][:, e, :],
+                            prod[c][:, e, 1 - c, halves[h]],
+                            ident[:],
+                            start=(c == 0),
+                            stop=(c == 1),
+                            is_transpose=True,
+                        )
+            for h in range(QH):
+                nc.vector.tensor_tensor(
+                    x_words[:, 1, halves[h]].bitcast(BF16).rearrange("p (q e) -> p q e", e=2),
+                    prod[0][:, :, 0, halves[h]].rearrange("p e q -> p q e"),
+                    prod[1][:, :, 1, halves[h]].rearrange("p e q -> p q e"),
+                    SUB,
+                )
+            for h in range(QH):
+                turn_back("z_turned1%d" % h, fwd[h][:], z_back[:, 1, halves[h]])
 
-        all_codes = keep.tile([P, QH * 2 * P], U32, name="codes", tag="word_tab0", align_bytes=64)
+        load_rel(0, 0, 2)
+        nc.sync.dma_start(rel_list[:], offs2)
+        load_rel(1, 0, 2)
+        nc.sync.dma_start(tail_list[:], offs3)
+        load_scales(0)
+        nc.sync.dma_start(head_list[:], offs)
+        load_head(0, 0, 2)
+        load_scales(1)
+        load_head(1, 0, 2)
+        load_rel(0, 2, 2)
+        load_rel(1, 2, 1)
+        load_head(0, 2, 1)
+        load_head(1, 2, 1)
+        load_rel(1, 3, 1)
+        load_head(0, 3, 1)
+        first_pair()
+        pick_scales(0)
+        pick_scales(1)
+        place_scales(0)
+        load_head(1, 3, 1)
+        place_scales(1)
+        load_words(0)
+        place_scales(2)
+        place_scales(3)
+        load_words(1)
+        second_pair()
+
+        tre_picked = keep.tile([P, I], U32, name="tre_picked", align_bytes=64)
+        nc.vector.tensor_copy(tre_picked[:], word_tab[0][:].bitcast(U32).indirect(tail_list[:]))
+        picked_words = {(0, j): tre_picked[:, j * IW : (j + 1) * IW] for j in range(IH)}
+
         codes = []
         scales = []
-        for h in range(QH):
-            grouped = keep.tile([P, 2 * P * PACK], BF16, name="grouped%d" % h, align_bytes=64)
+        for w in range(2):
+            grouped = keep.tile([P, Q * PACK], BF16, name="grouped%d" % w, tag="grouped%d" % w, align_bytes=64)
             nc.scalar.copy(
-                grouped[:].bitcast(F32).rearrange("p (w q u) -> p w q u", w=2, u=2),
-                back[h][:].rearrange("p w u q -> p w q u"),
+                grouped[:].bitcast(F32).rearrange("p (q u) -> p q u", u=2),
+                (x_words, z_back)[w][:].rearrange("p u q -> p q u"),
             )
-            cd = all_codes[:, h * 2 * P : (h + 1) * 2 * P]
-            sc = keep.tile([P, 2 * P], U8, name="scales%d" % h, align_bytes=64)
-            nc.vector.quantize_mx(out=cd.bitcast(FP8X4), scales=sc[:], in_=grouped[:])
+            cd = keep.tile([P, Q], U32, name="codes%d" % w, tag=("word_tab0", "grouped0")[w], align_bytes=64)
+            sc = keep.tile([P, Q], U8, name="scales%d" % w, align_bytes=64)
+            nc.vector.quantize_mx(out=cd[:].bitcast(FP8X4), scales=sc[:], in_=grouped[:])
             codes.append(cd)
             scales.append(sc)
 
-        def mx_pass(acc, h, w, cols):
+        def mx_pass(acc, h, w, j):
             nc.tensor.matmul_mx(
                 out=acc[:],
-                lhsT=codes[h][:, w * P : (w + 1) * P].bitcast(FP8X4),
-                lhsT_scale=scales[h][:, w * P : (w + 1) * P],
-                rhs=picked_words[w][:, cols].bitcast(FP8X4),
-                rhs_scale=tail_scales[:, w * I + cols.start : w * I + cols.stop],
+                lhsT=codes[w][:, halves[h]].bitcast(FP8X4),
+                lhsT_scale=scales[w][:, halves[h]],
+                rhs=picked_words[w, j].bitcast(FP8X4),
+                rhs_scale=tail_scales[:, w * I + j * IW : w * I + (j + 1) * IW],
                 start=(w == 0),
                 stop=(w == 1),
             )
@@ -186,17 +232,18 @@ def tile_attend_complexscores_kernel(
         for h in range(QH):
             for j in range(IH):
                 accs[j, h] = psum.tile([P, IW], F32, name="acc%d%d" % (j, h), tag="bank%d%d" % (h, j))
-                mx_pass(accs[j, h], h, 0, slice(j * IW, (j + 1) * IW))
+                mx_pass(accs[j, h], h, 0, j)
         for j in range(IH):
-            cols = slice(j * IW, (j + 1) * IW)
+            tim_picked = keep.tile([P, IW], U32, name="tim_picked%d" % j, align_bytes=64)
+            picked_words[1, j] = tim_picked[:]
             nc.vector.tensor_copy(
-                picked_words[1][:, cols],
+                tim_picked[:],
                 word_tab[1][:].bitcast(U32).indirect(tail_list[:, j * IW // 16 : (j + 1) * IW // 16]),
             )
         for j in range(IH):
             cols = slice(j * IW, (j + 1) * IW)
             for h in range(QH):
-                mx_pass(accs[j, h], h, 1, cols)
+                mx_pass(accs[j, h], h, 1, j)
                 result = keep.tile([P, IW], F32, name="result%d%d" % (j, h))
                 if j == IH - 1 and h == QH - 1:
                     nc.vector.tensor_copy(result[:], accs[j, h][:])

@@ -66,16 +66,17 @@ def tile_attend_complexscores_kernel(
 
         def load_scales(c):
             src = (tre_scales, tim_scales)[c]
-            nc.sync.dma_start(out=scale_tab[c][0:P:8, :].bitcast(I32), in_=src[0].bitcast(I32))
+            nc.sync.dma_start(out=scale_tab[c][32:96:4, :].bitcast(I32), in_=src[0].bitcast(I32))
 
         picked_scales = keep.tile([P, 2 * I], U8, name="picked_scales")
 
         def pick_scales(c):
             nc.vector.tensor_copy(picked_scales[:, c * I : (c + 1) * I], scale_tab[c][:].indirect(tail_list[:]))
 
-        def place_scales(j):
+        def place_scales(c, r):
+            cols = slice(c * I, (c + 1) * I)
             nc.sync.dma_start(
-                out=tail_scales[j:P:32, :].bitcast(I32), in_=picked_scales[8 * j : P : 32, :].bitcast(I32)
+                out=tail_scales[r:P:32, cols].bitcast(I32), in_=picked_scales[32 + 4 * r : 96 : 16, cols].bitcast(I32)
             )
 
         def load_words(c):
@@ -136,7 +137,7 @@ def tile_attend_complexscores_kernel(
                 turn_back("z_turned0%d" % h, fwd[h, 1][:], z_back[:, 0, halves[h]])
 
         def second_pair():
-            fwd = [psum.tile([P, 2, P], F32, name="z_fwd%d" % h) for h in range(QH)]
+            fwd = [psum.tile([P, 2, P], F32, name="z_fwd%d" % h, tag="z_fwd%d" % h) for h in range(QH)]
             prod = [keep.tile([P, 2, 2, Q], F32, name="prod%d" % c) for c in range(2)]
             for e in range(2):
                 t = 2 + e
@@ -190,13 +191,15 @@ def tile_attend_complexscores_kernel(
         first_pair()
         pick_scales(0)
         pick_scales(1)
-        place_scales(0)
+        place_scales(0, 0)
         load_head(1, 3, 1)
-        place_scales(1)
+        place_scales(0, 1)
         load_words(0)
-        place_scales(2)
-        place_scales(3)
+        place_scales(0, 2)
+        place_scales(0, 3)
         load_words(1)
+        for r in range(4):
+            place_scales(1, r)
         second_pair()
 
         tre_picked = keep.tile([P, I], U32, name="tre_picked", align_bytes=64)
@@ -217,22 +220,29 @@ def tile_attend_complexscores_kernel(
             codes.append(cd)
             scales.append(sc)
 
-        def mx_pass(acc, h, w, j):
+        def mx_pass(acc, h, w, first, width):
+            j, lo = divmod(first, IW)
             nc.tensor.matmul_mx(
                 out=acc[:],
                 lhsT=codes[w][:, halves[h]].bitcast(FP8X4),
                 lhsT_scale=scales[w][:, halves[h]],
-                rhs=picked_words[w, j].bitcast(FP8X4),
-                rhs_scale=tail_scales[:, w * I + j * IW : w * I + (j + 1) * IW],
+                rhs=picked_words[w, j][:, lo : lo + width].bitcast(FP8X4),
+                rhs_scale=tail_scales[:, w * I + first : w * I + first + width],
                 start=(w == 0),
                 stop=(w == 1),
             )
 
-        accs = {}
-        for h in range(QH):
-            for j in range(IH):
-                accs[j, h] = psum.tile([P, IW], F32, name="acc%d%d" % (j, h), tag="bank%d%d" % (h, j))
-                mx_pass(accs[j, h], h, 0, j)
+        pieces = [
+            (0, 0, P, nc.scalar.copy, "bank00"),
+            (0, P, P, nc.scalar.copy, "z_fwd1"),
+            (1, 0, IW, nc.vector.tensor_copy, "bank10"),
+            (0, IW, IW, nc.scalar.copy, "bank01"),
+            (1, IW, IW, nc.vector.tensor_copy, "bank11"),
+        ]
+        accs = []
+        for k, (h, first, width, engine, tag) in enumerate(pieces):
+            accs.append(psum.tile([P, width], F32, name="acc%d" % k, tag=tag))
+            mx_pass(accs[k], h, 0, first, width)
         for j in range(IH):
             tim_picked = keep.tile([P, IW], U32, name="tim_picked%d" % j, align_bytes=64)
             picked_words[1, j] = tim_picked[:]
@@ -240,13 +250,8 @@ def tile_attend_complexscores_kernel(
                 tim_picked[:],
                 word_tab[1][:].bitcast(U32).indirect(tail_list[:, j * IW // 16 : (j + 1) * IW // 16]),
             )
-        for j in range(IH):
-            cols = slice(j * IW, (j + 1) * IW)
-            for h in range(QH):
-                mx_pass(accs[j, h], h, 1, j)
-                result = keep.tile([P, IW], F32, name="result%d%d" % (j, h))
-                if j == IH - 1 and h == QH - 1:
-                    nc.vector.tensor_copy(result[:], accs[j, h][:])
-                else:
-                    nc.scalar.copy(result[:], accs[j, h][:])
-                nc.sync.dma_start(out=out[h * P : (h + 1) * P, cols], in_=result[:])
+        for k, (h, first, width, engine, tag) in enumerate(pieces):
+            mx_pass(accs[k], h, 1, first, width)
+            result = keep.tile([P, width], F32, name="result%d" % k)
+            engine(result[:], accs[k][:])
+            nc.sync.dma_start(out=out[halves[h], first : first + width], in_=result[:])

@@ -68,15 +68,18 @@ def tile_attend_complexscores_kernel(
             src = (tre_scales, tim_scales)[c]
             nc.sync.dma_start(out=scale_tab[c][32:96:4, :].bitcast(I32), in_=src[0].bitcast(I32))
 
-        picked_scales = keep.tile([P, 2 * I], U8, name="picked_scales")
+        picked_scales = [
+            keep.tile([P, I], U8, name="picked_scales%d" % c, tag="picked_scales%d" % c, align_bytes=64)
+            for c in range(2)
+        ]
 
         def pick_scales(c):
-            nc.vector.tensor_copy(picked_scales[:, c * I : (c + 1) * I], scale_tab[c][:].indirect(tail_list[:]))
+            nc.vector.tensor_copy(picked_scales[c][:], scale_tab[c][:].indirect(tail_list[:]))
 
         def place_scales(c, r):
             cols = slice(c * I, (c + 1) * I)
             nc.sync.dma_start(
-                out=tail_scales[r:P:32, cols].bitcast(I32), in_=picked_scales[32 + 4 * r : 96 : 16, cols].bitcast(I32)
+                out=tail_scales[r:P:32, cols].bitcast(I32), in_=picked_scales[c][32 + 4 * r : 96 : 16, :].bitcast(I32)
             )
 
         def load_words(c):
@@ -208,15 +211,15 @@ def tile_attend_complexscores_kernel(
 
         codes = []
         scales = []
+        grouped = keep.tile([P, 2, Q * PACK], BF16, name="grouped", tag="picked_scales0", align_bytes=64)
         for w in range(2):
-            grouped = keep.tile([P, Q * PACK], BF16, name="grouped%d" % w, tag="grouped%d" % w, align_bytes=64)
             nc.scalar.copy(
-                grouped[:].bitcast(F32).rearrange("p (q u) -> p q u", u=2),
+                grouped[:, w, :].bitcast(F32).rearrange("p (q u) -> p q u", u=2),
                 (x_words, z_back)[w][:].rearrange("p u q -> p q u"),
             )
-            cd = keep.tile([P, Q], U32, name="codes%d" % w, tag=("word_tab0", "grouped0")[w], align_bytes=64)
+            cd = keep.tile([P, Q], U32, name="codes%d" % w, align_bytes=64)
             sc = keep.tile([P, Q], U8, name="scales%d" % w, align_bytes=64)
-            nc.vector.quantize_mx(out=cd[:].bitcast(FP8X4), scales=sc[:], in_=grouped[:])
+            nc.vector.quantize_mx(out=cd[:].bitcast(FP8X4), scales=sc[:], in_=grouped[:, w, :])
             codes.append(cd)
             scales.append(sc)
 

@@ -147,7 +147,7 @@ def tile_attend_complexscores_kernel(
                 rel = keep.tile([P, 2, Q], F32, name="rel%d" % t)
                 gather_rel(t, rel[:])
                 for c in range(2):
-                    last = (e, c) == (1, 1)
+                    last = e == 1
                     head = gather_head(c, t, QH if last else 1)
                     engine = nc.vector if e == 1 else nc.gpsimd
                     for cols in halves if last else [slice(0, Q)]:
@@ -157,13 +157,15 @@ def tile_attend_complexscores_kernel(
                             rel[:, :, cols],
                             MULT,
                         )
+            for c in range(2):
+                for e in range(2):
                     for h in range(QH):
                         nc.tensor.matmul(
                             fwd[h][:, e, :],
                             prod[c][:, e, 1 - c, halves[h]],
                             ident[:],
-                            start=(c == 0),
-                            stop=(c == 1),
+                            start=(c, e) == (0, 0),
+                            stop=(c, e) == (1, 1),
                             is_transpose=True,
                         )
             for h in range(QH):
@@ -194,8 +196,8 @@ def tile_attend_complexscores_kernel(
         first_pair()
         pick_scales(0)
         pick_scales(1)
-        place_scales(0, 0)
         load_head(1, 3, 1)
+        place_scales(0, 0)
         place_scales(0, 1)
         load_words(0)
         place_scales(0, 2)

@@ -86,7 +86,9 @@ def tile_attend_complexscores_kernel(
             src = (tre_words, tim_words)[c]
             nc.sync.dma_start(out=word_tab[c][:], in_=src[0].rearrange("p n t -> p (n t)").bitcast(I32))
 
-        x_words = keep.tile([P, 2, Q], F32, name="x_words")
+        x_words = [
+            keep.tile([P, 2, P], F32, name="x_words%d" % h, tag="x_words%d" % h, align_bytes=64) for h in range(QH)
+        ]
         x_back = psum.tile([P, Q], F32, name="x_back")
         z_back = psum.tile([P, 2, Q], F32, name="z_back")
         halves = [slice(h * P, (h + 1) * P) for h in range(QH)]
@@ -135,7 +137,8 @@ def tile_attend_complexscores_kernel(
                             )
             for h in range(QH):
                 turn_back("x_turned%d" % h, fwd[h, 0][:], x_back[:, halves[h]])
-            nc.scalar.copy(x_words[:, 0, :], x_back[:])
+            for h in range(QH):
+                nc.scalar.copy(x_words[h][:, 0, :], x_back[:, halves[h]])
             for h in range(QH):
                 turn_back("z_turned0%d" % h, fwd[h, 1][:], z_back[:, 0, halves[h]])
 
@@ -170,7 +173,7 @@ def tile_attend_complexscores_kernel(
                         )
             for h in range(QH):
                 nc.vector.tensor_tensor(
-                    x_words[:, 1, halves[h]].bitcast(BF16).rearrange("p (q e) -> p q e", e=2),
+                    x_words[h][:, 1, :].bitcast(BF16).rearrange("p (q e) -> p q e", e=2),
                     prod[0][:, :, 0, halves[h]].rearrange("p e q -> p q e"),
                     prod[1][:, :, 1, halves[h]].rearrange("p e q -> p q e"),
                     SUB,
@@ -207,30 +210,41 @@ def tile_attend_complexscores_kernel(
             place_scales(1, r)
         second_pair()
 
-        tre_picked = keep.tile([P, I], U32, name="tre_picked", align_bytes=64)
-        nc.vector.tensor_copy(tre_picked[:], word_tab[0][:].bitcast(U32).indirect(tail_list[:]))
-        picked_words = {(0, j): tre_picked[:, j * IW : (j + 1) * IW] for j in range(IH)}
+        picked_words = {}
 
-        codes = []
-        scales = []
-        grouped = keep.tile([P, 2, Q * PACK], BF16, name="grouped", tag="picked_scales0", align_bytes=64)
-        for w in range(2):
-            nc.scalar.copy(
-                grouped[:, w, :].bitcast(F32).rearrange("p (q u) -> p q u", u=2),
-                (x_words, z_back)[w][:].rearrange("p u q -> p q u"),
+        def pick_words(w, j, tag):
+            picked = keep.tile([P, IW], U32, name="picked_words%d%d" % (w, j), tag=tag, align_bytes=64)
+            nc.vector.tensor_copy(
+                picked[:], word_tab[w][:].bitcast(U32).indirect(tail_list[:, j * IW // 16 : (j + 1) * IW // 16])
             )
-            cd = keep.tile([P, Q], U32, name="codes%d" % w, align_bytes=64)
-            sc = keep.tile([P, Q], U8, name="scales%d" % w, align_bytes=64)
-            nc.vector.quantize_mx(out=cd[:].bitcast(FP8X4), scales=sc[:], in_=grouped[:, w, :])
-            codes.append(cd)
-            scales.append(sc)
+            picked_words[w, j] = picked[:]
+
+        grouped = keep.tile([P, 2, Q * PACK], BF16, name="grouped", tag="picked_scales0", align_bytes=64)
+        codes = {}
+        scales = {}
+
+        def quantise(w, first, width, pairs):
+            source = grouped[:, w, first * PACK : (first + width) * PACK]
+            nc.scalar.copy(source.bitcast(F32).rearrange("p (q u) -> p q u", u=2), pairs.rearrange("p u q -> p q u"))
+            cd = keep.tile([P, width], U32, name="codes%d%d" % (w, first), align_bytes=64)
+            sc = keep.tile([P, width], U8, name="scales%d%d" % (w, first), align_bytes=64)
+            nc.vector.quantize_mx(out=cd[:].bitcast(FP8X4), scales=sc[:], in_=source)
+            for lo in range(0, width, P):
+                codes[w, (first + lo) // P] = cd[:, lo : lo + P]
+                scales[w, (first + lo) // P] = sc[:, lo : lo + P]
+
+        pick_words(0, 0, "picked_words00")
+        quantise(0, 0, P, x_words[0][:])
+        pick_words(0, 1, "x_words0")
+        quantise(0, P, P, x_words[1][:])
+        quantise(1, 0, Q, z_back[:])
 
         def mx_pass(acc, h, w, first, width):
             j, lo = divmod(first, IW)
             nc.tensor.matmul_mx(
                 out=acc[:],
-                lhsT=codes[w][:, halves[h]].bitcast(FP8X4),
-                lhsT_scale=scales[w][:, halves[h]],
+                lhsT=codes[w, h].bitcast(FP8X4),
+                lhsT_scale=scales[w, h],
                 rhs=picked_words[w, j][:, lo : lo + width].bitcast(FP8X4),
                 rhs_scale=tail_scales[:, w * I + first : w * I + first + width],
                 start=(w == 0),
@@ -247,14 +261,12 @@ def tile_attend_complexscores_kernel(
         accs = []
         for k, (h, first, width, engine, tag) in enumerate(pieces):
             accs.append(psum.tile([P, width], F32, name="acc%d" % k, tag=tag))
-            mx_pass(accs[k], h, 0, first, width)
+        for half in range(QH):
+            for k, (h, first, width, engine, tag) in enumerate(pieces):
+                if h == half:
+                    mx_pass(accs[k], h, 0, first, width)
         for j in range(IH):
-            tim_picked = keep.tile([P, IW], U32, name="tim_picked%d" % j, align_bytes=64)
-            picked_words[1, j] = tim_picked[:]
-            nc.vector.tensor_copy(
-                tim_picked[:],
-                word_tab[1][:].bitcast(U32).indirect(tail_list[:, j * IW // 16 : (j + 1) * IW // 16]),
-            )
+            pick_words(1, j, "picked_words1%d" % j)
         for k, (h, first, width, engine, tag) in enumerate(pieces):
             mx_pass(accs[k], h, 1, first, width)
             result = keep.tile([P, width], F32, name="result%d" % k)

@@ -233,10 +233,12 @@ def tile_attend_complexscores_kernel(
                 codes[w, (first + lo) // P] = cd[:, lo : lo + P]
                 scales[w, (first + lo) // P] = sc[:, lo : lo + P]
 
-        pick_words(0, 0, "picked_words00")
-        quantise(0, 0, P, x_words[0][:])
-        pick_words(0, 1, "x_words0")
-        quantise(0, P, P, x_words[1][:])
+        tre_picked = keep.tile([P, I], U32, name="tre_picked", align_bytes=64)
+        nc.vector.tensor_copy(tre_picked[:], word_tab[0][:].bitcast(U32).indirect(tail_list[:]))
+        for j in range(IH):
+            picked_words[0, j] = tre_picked[:, j * IW : (j + 1) * IW]
+        for h in range(QH):
+            quantise(0, h * P, P, x_words[h][:])
         quantise(1, 0, Q, z_back[:])
 
         def mx_pass(acc, h, w, first, width):

@@ -15,13 +15,13 @@ U8 = mybir.dt.uint8
 FP8X4 = mybir.dt.float8_e4m3fn_x4
 MULT = mybir.AluOpType.mult
 SUB = mybir.AluOpType.subtract
+COPY = mybir.ActivationFunctionType.Copy
 
 P = 128
 PACK = 4
 QH = Q // P
 IH = 2
 IW = I // IH
-ROWS = D // 32
 
 
 def tile_attend_complexscores_kernel(
@@ -43,9 +43,7 @@ def tile_attend_complexscores_kernel(
         nc.vector.memset(tail_scales[:].bitcast(I32), 0)
         ident = keep.tile([P, P], F32, name="ident")
         make_identity(nc, ident[:])
-        word_tab = [
-            keep.tile([P, V], I32, name="word_tab%d" % c, tag="word_tab%d" % c, align_bytes=64) for c in range(2)
-        ]
+        word_tab = [keep.tile([P, V], I32, name="word_tab%d" % c, align_bytes=64) for c in range(2)]
 
         rel_src = [src.rearrange("(p t) u -> p (t u)", t=PACK) for src in (rre, rim)]
         head_src = [src.rearrange("(p t) n -> p (t n)", t=PACK) for src in (hre, him)]
@@ -55,11 +53,12 @@ def tile_attend_complexscores_kernel(
         def load_rel(c, t, n):
             tab = keep.tile([P, n * U], F32, name="rel_tab%d%d" % (c, t))
             nc.sync.dma_start(out=tab[:], in_=rel_src[c][:, t * U : (t + n) * U])
-            for e in range(n):
+            rel_tab[c, t] = tab[:]
+            for e in range(1, n):
                 rel_tab[c, t + e] = tab[:, e * U : (e + 1) * U]
 
         def load_head(c, t, n):
-            tab = keep.tile([P, n * T], F32, name="head_tab%d%d" % (c, t))
+            tab = keep.tile([P, n * T], F32, name="head_tab%d%d" % (c, t), tag="head_tab%d%d" % (c, t))
             nc.sync.dma_start(out=tab[:], in_=head_src[c][:, t * T : (t + n) * T])
             for e in range(n):
                 head_tab[c, t + e] = tab[:, e * T : (e + 1) * T]
@@ -86,102 +85,67 @@ def tile_attend_complexscores_kernel(
             src = (tre_words, tim_words)[c]
             nc.sync.dma_start(out=word_tab[c][:], in_=src[0].rearrange("p n t -> p (n t)").bitcast(I32))
 
-        x_words = [
-            keep.tile([P, 2, P], F32, name="x_words%d" % h, tag="x_words%d" % h, align_bytes=64) for h in range(QH)
-        ]
-        x_back = psum.tile([P, Q], F32, name="x_back")
-        z_back = psum.tile([P, 2, Q], F32, name="z_back")
         halves = [slice(h * P, (h + 1) * P) for h in range(QH)]
+        rel = [keep.tile([P, 2, Q], F32, name="rel%d" % t) for t in range(PACK)]
 
-        def turn_back(name, summed, back):
-            turned = keep.tile([P, P, 2], BF16, name=name)
-            nc.scalar.copy(turned[:], summed.rearrange("q e p -> q p e"))
-            nc.tensor.transpose(back, turned[:].rearrange("q p e -> q (p e)").bitcast(F32), ident[:])
+        def scalar_gather(dst, window):
+            nc.scalar.activation(dst, window, COPY)
 
-        def gather_rel(t, rel):
-            for c in range(2):
-                nc.vector.tensor_copy(rel[:, c, :], rel_tab[c, t].indirect(rel_list[:]))
+        def gather_rel(c, first, n):
+            scalar_gather(rel[first][:, c, :], rel_tab[c, first].indirect(rel_list[:]))
+            for t in range(first + 1, first + n):
+                nc.vector.tensor_copy(rel[t][:, c, :], rel_tab[c, t].indirect(rel_list[:]))
 
-        def gather_head(c, t, pieces):
-            head = keep.tile([P, 1, Q], F32, name="head%d%d" % (c, t))
-            width = Q // pieces
-            for k in range(pieces):
-                nc.vector.tensor_copy(
-                    head[:, 0, k * width : (k + 1) * width],
-                    head_tab[c, t].indirect(head_list[:, k * width // 16 : (k + 1) * width // 16]),
+        prod = {}
+        for c in range(2):
+            for u in range(2):
+                prod[c, u] = keep.tile([P, 2, 2, Q], F32, name="prod%d%d" % (c, u))
+
+        def multiply(c, t, gathers, engine):
+            width = Q // len(gathers)
+            for k, gather in enumerate(gathers):
+                cols = slice(k * width, (k + 1) * width)
+                head = keep.tile([P, 1, width], F32, name="head%d%d%d" % (c, t, k))
+                gather(head[:, 0, :], head_tab[c, t].indirect(head_list[:, cols.start // 16 : cols.stop // 16]))
+                engine.tensor_tensor(
+                    prod[c, t // 2][:, t % 2, :, cols], head[:].to_broadcast([P, 2, width]), rel[t][:, :, cols], MULT
                 )
-            return head
 
-        def first_pair():
-            fwd = {}
-            for h in range(QH):
-                for w in range(2):
-                    fwd[h, w] = psum.tile([P, 2, P], F32, name="fwd%d%d" % (h, w), tag="bank%d%d" % (h, w))
-            for t in range(2):
-                rel = keep.tile([P, 3, Q], F32, name="rel%d" % t)
-                gather_rel(t, rel[:, 1:3, :])
-                nc.scalar.mul(rel[:, 0, :], rel[:, 2, :], -1.0)
-                for c in range(2):
-                    head = gather_head(c, t, 1)
-                    prod = keep.tile([P, 2, Q], F32, name="prod%d%d" % (c, t))
-                    nc.gpsimd.tensor_tensor(prod[:], head[:].to_broadcast([P, 2, Q]), rel[:, 1 - c : 3 - c, :], MULT)
-                    for h in range(QH):
-                        for w in range(2):
-                            nc.tensor.matmul(
-                                fwd[h, w][:, t, :],
-                                prod[:, w, h * P : (h + 1) * P],
-                                ident[:],
-                                start=(c == 0),
-                                stop=(c == 1),
-                                is_transpose=True,
-                            )
-            for h in range(QH):
-                turn_back("x_turned%d" % h, fwd[h, 0][:], x_back[:, halves[h]])
-            for h in range(QH):
-                nc.scalar.copy(x_words[h][:, 0, :], x_back[:, halves[h]])
-            for h in range(QH):
-                turn_back("z_turned0%d" % h, fwd[h, 1][:], z_back[:, 0, halves[h]])
+        x_pairs = [keep.tile([P, 2, P], F32, name="x_pairs%d" % h, align_bytes=64) for h in range(QH)]
+        z_back = psum.tile([P, 2, Q], F32, name="z_back")
 
-        def second_pair():
-            fwd = [psum.tile([P, 2, P], F32, name="z_fwd%d" % h, tag="z_fwd%d" % h) for h in range(QH)]
-            prod = [keep.tile([P, 2, 2, Q], F32, name="prod%d" % c) for c in range(2)]
-            for e in range(2):
-                t = 2 + e
-                rel = keep.tile([P, 2, Q], F32, name="rel%d" % t)
-                gather_rel(t, rel[:])
-                for c in range(2):
-                    last = e == 1
-                    head = gather_head(c, t, QH if last else 1)
-                    engine = nc.vector if e == 1 else nc.gpsimd
-                    for cols in halves if last else [slice(0, Q)]:
-                        engine.tensor_tensor(
-                            prod[c][:, e, :, cols],
-                            head[:, :, cols].to_broadcast([P, 2, cols.stop - cols.start]),
-                            rel[:, :, cols],
-                            MULT,
-                        )
+        def subtract_x(u):
+            for h in range(QH):
+                nc.vector.tensor_tensor(
+                    x_pairs[h][:, u, :].bitcast(BF16).rearrange("p (q e) -> p q e", e=2),
+                    prod[0, u][:, :, 0, halves[h]].rearrange("p e q -> p q e"),
+                    prod[1, u][:, :, 1, halves[h]].rearrange("p e q -> p q e"),
+                    SUB,
+                )
+
+        def add_z(u):
+            fwd = [psum.tile([P, 2, P], F32, name="z_fwd%d%d" % (u, h), tag="z_fwd%d%d" % (u, h)) for h in range(QH)]
             for c in range(2):
                 for e in range(2):
                     for h in range(QH):
                         nc.tensor.matmul(
                             fwd[h][:, e, :],
-                            prod[c][:, e, 1 - c, halves[h]],
+                            prod[c, u][:, e, 1 - c, halves[h]],
                             ident[:],
                             start=(c, e) == (0, 0),
                             stop=(c, e) == (1, 1),
                             is_transpose=True,
                         )
-            for h in range(QH):
-                nc.vector.tensor_tensor(
-                    x_words[h][:, 1, :].bitcast(BF16).rearrange("p (q e) -> p q e", e=2),
-                    prod[0][:, :, 0, halves[h]].rearrange("p e q -> p q e"),
-                    prod[1][:, :, 1, halves[h]].rearrange("p e q -> p q e"),
-                    SUB,
-                )
-            for h in range(QH):
-                turn_back("z_turned1%d" % h, fwd[h][:], z_back[:, 1, halves[h]])
+            return fwd
 
-        load_rel(0, 0, 2)
+        def turn_back(u, fwd, turned):
+            for h in range(QH):
+                nc.scalar.copy(turned[h], fwd[h][:].rearrange("q e p -> q p e"))
+                nc.tensor.transpose(
+                    z_back[:, u, halves[h]], turned[h].rearrange("q p e -> q (p e)").bitcast(F32), ident[:]
+                )
+
+        load_rel(0, 0, 4)
         nc.sync.dma_start(rel_list[:], offs2)
         load_rel(1, 0, 2)
         nc.sync.dma_start(tail_list[:], offs3)
@@ -190,16 +154,20 @@ def tile_attend_complexscores_kernel(
         load_head(0, 0, 2)
         load_scales(1)
         load_head(1, 0, 2)
-        load_rel(0, 2, 2)
-        load_rel(1, 2, 1)
-        load_head(0, 2, 1)
+        load_rel(1, 2, 2)
+        load_head(0, 2, 2)
         load_head(1, 2, 1)
-        load_rel(1, 3, 1)
-        load_head(0, 3, 1)
-        first_pair()
+        load_head(1, 3, 1)
+        gather_rel(0, 0, 4)
+        gather_rel(1, 0, 2)
         pick_scales(0)
         pick_scales(1)
-        load_head(1, 3, 1)
+        for c in range(2):
+            for t in range(2):
+                multiply(c, t, [scalar_gather], nc.vector)
+        subtract_x(0)
+        first_sums = add_z(0)
+        gather_rel(1, 2, 2)
         place_scales(0, 0)
         place_scales(0, 1)
         load_words(0)
@@ -208,12 +176,20 @@ def tile_attend_complexscores_kernel(
         load_words(1)
         for r in range(4):
             place_scales(1, r)
-        second_pair()
+        multiply(0, 2, [scalar_gather], nc.vector)
+        multiply(0, 3, [nc.vector.tensor_copy], nc.vector)
+        multiply(1, 2, [scalar_gather], nc.vector)
+        multiply(1, 3, [nc.vector.tensor_copy, scalar_gather], nc.vector)
+        first_turned = keep.tile([P, QH, P, 2], BF16, name="first_turned", tag="head_tab13")
+        turn_back(0, first_sums, [first_turned[:, h] for h in range(QH)])
+        second_sums = add_z(1)
+        subtract_x(1)
+        turn_back(1, second_sums, [keep.tile([P, P, 2], BF16, name="turned%d" % h)[:] for h in range(QH)])
 
         picked_words = {}
 
-        def pick_words(w, j, tag):
-            picked = keep.tile([P, IW], U32, name="picked_words%d%d" % (w, j), tag=tag, align_bytes=64)
+        def pick_words(w, j):
+            picked = keep.tile([P, IW], U32, name="picked_words%d%d" % (w, j), align_bytes=64)
             nc.vector.tensor_copy(
                 picked[:], word_tab[w][:].bitcast(U32).indirect(tail_list[:, j * IW // 16 : (j + 1) * IW // 16])
             )
@@ -238,7 +214,7 @@ def tile_attend_complexscores_kernel(
         for j in range(IH):
             picked_words[0, j] = tre_picked[:, j * IW : (j + 1) * IW]
         for h in range(QH):
-            quantise(0, h * P, P, x_words[h][:])
+            quantise(0, h * P, P, x_pairs[h][:])
         quantise(1, 0, Q, z_back[:])
 
         def mx_pass(acc, h, w, first, width):
@@ -254,11 +230,11 @@ def tile_attend_complexscores_kernel(
             )
 
         pieces = [
-            (0, 0, P, nc.scalar.copy, "bank00"),
-            (0, P, P, nc.scalar.copy, "z_fwd1"),
-            (1, 0, IW, nc.vector.tensor_copy, "bank10"),
-            (0, IW, IW, nc.scalar.copy, "bank01"),
-            (1, IW, IW, nc.vector.tensor_copy, "bank11"),
+            (0, 0, P, nc.scalar.copy, "acc0"),
+            (0, P, P, nc.scalar.copy, "acc1"),
+            (1, 0, IW, nc.vector.tensor_copy, "z_fwd00"),
+            (0, IW, IW, nc.scalar.copy, "acc3"),
+            (1, IW, IW, nc.vector.tensor_copy, "z_fwd01"),
         ]
         accs = []
         for k, (h, first, width, engine, tag) in enumerate(pieces):
@@ -268,7 +244,7 @@ def tile_attend_complexscores_kernel(
                 if h == half:
                     mx_pass(accs[k], h, 0, first, width)
         for j in range(IH):
-            pick_words(1, j, "picked_words1%d" % j)
+            pick_words(1, j)
         for k, (h, first, width, engine, tag) in enumerate(pieces):
             mx_pass(accs[k], h, 1, first, width)
             result = keep.tile([P, width], F32, name="result%d" % k)

@@ -112,7 +112,7 @@ def tile_attend_complexscores_kernel(
                 )
 
         x_pairs = [keep.tile([P, 2, P], F32, name="x_pairs%d" % h, align_bytes=64) for h in range(QH)]
-        z_back = psum.tile([P, 2, Q], F32, name="z_back")
+        z_back = [psum.tile([P, 2, P], F32, name="z_back%d" % h) for h in range(QH)]
 
         def subtract_x(u):
             for h in range(QH):
@@ -142,7 +142,7 @@ def tile_attend_complexscores_kernel(
             for h in range(QH):
                 nc.scalar.copy(turned[h], fwd[h][:].rearrange("q e p -> q p e"))
                 nc.tensor.transpose(
-                    z_back[:, u, halves[h]], turned[h].rearrange("q p e -> q (p e)").bitcast(F32), ident[:]
+                    z_back[h][:, u, :], turned[h].rearrange("q p e -> q (p e)").bitcast(F32), ident[:]
                 )
 
         load_rel(0, 0, 4)
@@ -215,7 +215,8 @@ def tile_attend_complexscores_kernel(
             picked_words[0, j] = tre_picked[:, j * IW : (j + 1) * IW]
         for h in range(QH):
             quantise(0, h * P, P, x_pairs[h][:])
-        quantise(1, 0, Q, z_back[:])
+        for h in range(QH):
+            quantise(1, h * P, P, z_back[h][:])
 
         def mx_pass(acc, h, w, first, width):
             j, lo = divmod(first, IW)
@@ -233,7 +234,7 @@ def tile_attend_complexscores_kernel(
             (0, 0, P, nc.scalar.copy, "acc0"),
             (0, P, P, nc.scalar.copy, "acc1"),
             (1, 0, IW, nc.vector.tensor_copy, "z_fwd00"),
-            (0, IW, IW, nc.scalar.copy, "acc3"),
+            (0, IW, IW, nc.scalar.copy, "z_fwd10"),
             (1, IW, IW, nc.vector.tensor_copy, "z_fwd01"),
         ]
         accs = []

@@ -30,6 +30,7 @@ def tile_attend_complexscores_kernel(
     nc = tc.nc
     with ExitStack() as ctx:
         keep = ctx.enter_context(tc.tile_pool(name="keep", bufs=1))
+        shared = ctx.enter_context(tc.tile_pool(name="shared", bufs=1))
         psum = ctx.enter_context(tc.psum_pool(name="psum", bufs=1))
 
         head_list = keep.tile([P, Q // 16], U16, name="head_list")
@@ -43,7 +44,10 @@ def tile_attend_complexscores_kernel(
         nc.vector.memset(tail_scales[:].bitcast(I32), 0)
         ident = keep.tile([P, P], F32, name="ident")
         make_identity(nc, ident[:])
-        word_tab = [keep.tile([P, V], I32, name="word_tab%d" % c, align_bytes=64) for c in range(2)]
+        word_tab = [
+            shared.tile([P, V], I32, name="word_tab0", align_bytes=64, offset=0),
+            keep.tile([P, V], I32, name="word_tab1", align_bytes=64),
+        ]
 
         rel_src = [src.rearrange("(p t) u -> p (t u)", t=PACK) for src in (rre, rim)]
         head_src = [src.rearrange("(p t) n -> p (t n)", t=PACK) for src in (hre, him)]
@@ -67,18 +71,14 @@ def tile_attend_complexscores_kernel(
             src = (tre_scales, tim_scales)[c]
             nc.sync.dma_start(out=scale_tab[c][32:96:4, :].bitcast(I32), in_=src[0].bitcast(I32))
 
-        picked_scales = [
-            keep.tile([P, I], U8, name="picked_scales%d" % c, tag="picked_scales%d" % c, align_bytes=64)
-            for c in range(2)
-        ]
+        picked_scales = keep.tile([P, 2 * I], U8, name="picked_scales", align_bytes=64)
 
         def pick_scales(c):
-            nc.vector.tensor_copy(picked_scales[c][:], scale_tab[c][:].indirect(tail_list[:]))
+            nc.vector.tensor_copy(picked_scales[:, c * I : (c + 1) * I], scale_tab[c][:].indirect(tail_list[:]))
 
-        def place_scales(c, r):
-            cols = slice(c * I, (c + 1) * I)
+        def place_scales(r):
             nc.sync.dma_start(
-                out=tail_scales[r:P:32, cols].bitcast(I32), in_=picked_scales[c][32 + 4 * r : 96 : 16, :].bitcast(I32)
+                out=tail_scales[r:P:32, :].bitcast(I32), in_=picked_scales[32 + 4 * r : 96 : 16, :].bitcast(I32)
             )
 
         def load_words(c):
@@ -156,8 +156,6 @@ def tile_attend_complexscores_kernel(
         load_head(1, 0, 2)
         load_rel(1, 2, 2)
         load_head(0, 2, 2)
-        load_head(1, 2, 1)
-        load_head(1, 3, 1)
         gather_rel(0, 0, 4)
         gather_rel(1, 0, 2)
         pick_scales(0)
@@ -168,14 +166,12 @@ def tile_attend_complexscores_kernel(
         subtract_x(0)
         first_sums = add_z(0)
         gather_rel(1, 2, 2)
-        place_scales(0, 0)
-        place_scales(0, 1)
-        load_words(0)
-        place_scales(0, 2)
-        place_scales(0, 3)
-        load_words(1)
         for r in range(4):
-            place_scales(1, r)
+            place_scales(r)
+        load_head(1, 2, 1)
+        load_head(1, 3, 1)
+        load_words(0)
+        load_words(1)
         multiply(0, 2, [scalar_gather], nc.vector)
         multiply(0, 3, [nc.vector.tensor_copy], nc.vector)
         multiply(1, 2, [scalar_gather], nc.vector)
@@ -195,14 +191,14 @@ def tile_attend_complexscores_kernel(
             )
             picked_words[w, j] = picked[:]
 
-        grouped = keep.tile([P, 2, Q * PACK], BF16, name="grouped", tag="picked_scales0", align_bytes=64)
+        grouped = keep.tile([P, 2, Q * PACK], BF16, name="grouped", align_bytes=64)
         codes = {}
         scales = {}
 
         def quantise(w, first, width, pairs):
             source = grouped[:, w, first * PACK : (first + width) * PACK]
             nc.scalar.copy(source.bitcast(F32).rearrange("p (q u) -> p q u", u=2), pairs.rearrange("p u q -> p q u"))
-            cd = keep.tile([P, width], U32, name="codes%d%d" % (w, first), align_bytes=64)
+            cd = shared.tile([P, width], U32, name="codes%d%d" % (w, first), align_bytes=64, offset=4 * (w * Q + first))
             sc = keep.tile([P, width], U8, name="scales%d%d" % (w, first), align_bytes=64)
             nc.vector.quantize_mx(out=cd[:].bitcast(FP8X4), scales=sc[:], in_=source)
             for lo in range(0, width, P):

@@ -20,7 +20,7 @@ COPY = mybir.ActivationFunctionType.Copy
 P = 128
 PACK = 4
 QH = Q // P
-IH = 2
+IH = 4
 IW = I // IH
 
 
@@ -30,7 +30,6 @@ def tile_attend_complexscores_kernel(
     nc = tc.nc
     with ExitStack() as ctx:
         keep = ctx.enter_context(tc.tile_pool(name="keep", bufs=1))
-        shared = ctx.enter_context(tc.tile_pool(name="shared", bufs=1))
         psum = ctx.enter_context(tc.psum_pool(name="psum", bufs=1))
 
         head_list = keep.tile([P, Q // 16], U16, name="head_list")
@@ -44,10 +43,7 @@ def tile_attend_complexscores_kernel(
         nc.vector.memset(tail_scales[:].bitcast(I32), 0)
         ident = keep.tile([P, P], F32, name="ident")
         make_identity(nc, ident[:])
-        word_tab = [
-            shared.tile([P, V], I32, name="word_tab0", align_bytes=64, offset=0),
-            keep.tile([P, V], I32, name="word_tab1", align_bytes=64),
-        ]
+        word_tab = [keep.tile([P, V], I32, name="word_tab%d" % c, align_bytes=64) for c in range(2)]
 
         rel_src = [src.rearrange("(p t) u -> p (t u)", t=PACK) for src in (rre, rim)]
         head_src = [src.rearrange("(p t) n -> p (t n)", t=PACK) for src in (hre, him)]
@@ -71,7 +67,7 @@ def tile_attend_complexscores_kernel(
             src = (tre_scales, tim_scales)[c]
             nc.sync.dma_start(out=scale_tab[c][32:96:4, :].bitcast(I32), in_=src[0].bitcast(I32))
 
-        picked_scales = keep.tile([P, 2 * I], U8, name="picked_scales", align_bytes=64)
+        picked_scales = keep.tile([P, 2 * I], U8, name="picked_scales", tag="picked_scales", align_bytes=64)
 
         def pick_scales(c):
             nc.vector.tensor_copy(picked_scales[:, c * I : (c + 1) * I], scale_tab[c][:].indirect(tail_list[:]))
@@ -112,7 +108,7 @@ def tile_attend_complexscores_kernel(
                 )
 
         x_pairs = [keep.tile([P, 2, P], F32, name="x_pairs%d" % h, align_bytes=64) for h in range(QH)]
-        z_back = [psum.tile([P, 2, P], F32, name="z_back%d" % h) for h in range(QH)]
+        z_back = [psum.tile([P, 2, P], F32, name="z_back%d" % h, tag="z_back%d" % h) for h in range(QH)]
 
         def subtract_x(u):
             for h in range(QH):
@@ -166,11 +162,12 @@ def tile_attend_complexscores_kernel(
         subtract_x(0)
         first_sums = add_z(0)
         gather_rel(1, 2, 2)
-        for r in range(4):
+        for r in range(3):
             place_scales(r)
         load_head(1, 2, 1)
         load_head(1, 3, 1)
         load_words(0)
+        place_scales(3)
         load_words(1)
         multiply(0, 2, [scalar_gather], nc.vector)
         multiply(0, 3, [nc.vector.tensor_copy], nc.vector)
@@ -182,23 +179,14 @@ def tile_attend_complexscores_kernel(
         subtract_x(1)
         turn_back(1, second_sums, [keep.tile([P, P, 2], BF16, name="turned%d" % h)[:] for h in range(QH)])
 
-        picked_words = {}
-
-        def pick_words(w, j):
-            picked = keep.tile([P, IW], U32, name="picked_words%d%d" % (w, j), align_bytes=64)
-            nc.vector.tensor_copy(
-                picked[:], word_tab[w][:].bitcast(U32).indirect(tail_list[:, j * IW // 16 : (j + 1) * IW // 16])
-            )
-            picked_words[w, j] = picked[:]
-
-        grouped = keep.tile([P, 2, Q * PACK], BF16, name="grouped", align_bytes=64)
+        grouped = keep.tile([P, 2, Q * PACK], BF16, name="grouped", tag="picked_scales", align_bytes=64)
         codes = {}
         scales = {}
 
         def quantise(w, first, width, pairs):
             source = grouped[:, w, first * PACK : (first + width) * PACK]
             nc.scalar.copy(source.bitcast(F32).rearrange("p (q u) -> p q u", u=2), pairs.rearrange("p u q -> p q u"))
-            cd = shared.tile([P, width], U32, name="codes%d%d" % (w, first), align_bytes=64, offset=4 * (w * Q + first))
+            cd = keep.tile([P, width], U32, name="codes%d%d" % (w, first), align_bytes=64)
             sc = keep.tile([P, width], U8, name="scales%d%d" % (w, first), align_bytes=64)
             nc.vector.quantize_mx(out=cd[:].bitcast(FP8X4), scales=sc[:], in_=source)
             for lo in range(0, width, P):
@@ -207,43 +195,56 @@ def tile_attend_complexscores_kernel(
 
         tre_picked = keep.tile([P, I], U32, name="tre_picked", align_bytes=64)
         nc.vector.tensor_copy(tre_picked[:], word_tab[0][:].bitcast(U32).indirect(tail_list[:]))
-        for j in range(IH):
-            picked_words[0, j] = tre_picked[:, j * IW : (j + 1) * IW]
         for h in range(QH):
             quantise(0, h * P, P, x_pairs[h][:])
         for h in range(QH):
             quantise(1, h * P, P, z_back[h][:])
 
-        def mx_pass(acc, h, w, first, width):
-            j, lo = divmod(first, IW)
+        def mx_pass(acc, h, w, words, first, start, stop):
+            width = acc.shape[-1]
             nc.tensor.matmul_mx(
-                out=acc[:],
+                out=acc,
                 lhsT=codes[w, h].bitcast(FP8X4),
                 lhsT_scale=scales[w, h],
-                rhs=picked_words[w, j][:, lo : lo + width].bitcast(FP8X4),
+                rhs=words.bitcast(FP8X4),
                 rhs_scale=tail_scales[:, w * I + first : w * I + first + width],
-                start=(w == 0),
-                stop=(w == 1),
+                start=start,
+                stop=stop,
             )
 
-        pieces = [
-            (0, 0, P, nc.scalar.copy, "acc0"),
-            (0, P, P, nc.scalar.copy, "acc1"),
-            (1, 0, IW, nc.vector.tensor_copy, "z_fwd00"),
-            (0, IW, IW, nc.scalar.copy, "z_fwd10"),
-            (1, IW, IW, nc.vector.tensor_copy, "z_fwd01"),
+        banks = [
+            (0, 0, 1, "acc0"),
+            (0, 1, 1, "acc1"),
+            (0, 2, 1, "z_fwd00"),
+            (0, 3, 1, "z_fwd01"),
+            (1, 0, 2, "z_fwd10"),
+            (1, 2, 1, "z_fwd11"),
+            (1, 3, 1, "z_back0"),
         ]
-        accs = []
-        for k, (h, first, width, engine, tag) in enumerate(pieces):
-            accs.append(psum.tile([P, width], F32, name="acc%d" % k, tag=tag))
-        for half in range(QH):
-            for k, (h, first, width, engine, tag) in enumerate(pieces):
-                if h == half:
-                    mx_pass(accs[k], h, 0, first, width)
-        for j in range(IH):
-            pick_words(1, j)
-        for k, (h, first, width, engine, tag) in enumerate(pieces):
-            mx_pass(accs[k], h, 1, first, width)
-            result = keep.tile([P, width], F32, name="result%d" % k)
-            engine(result[:], accs[k][:])
-            nc.sync.dma_start(out=out[halves[h], first : first + width], in_=result[:])
+        stores = [(0, 0, 1), (0, 1, 1), (1, 0, 2), (0, 2, 2), (1, 2, 2)]
+        empty = (nc.scalar.copy, nc.vector.tensor_copy)
+        accs = {}
+        for h, j, n, tag in banks:
+            accs[h, j] = psum.tile([P, n * IW], F32, name="acc%d%d" % (h, j), tag=tag)
+            mx_pass(accs[h, j][:], h, 0, tre_picked[:, j * IW : (j + n) * IW], j * IW, True, False)
+        results = {}
+        for h, j, n in stores:
+            results[h, j] = keep.tile([P, n * IW], F32, name="result%d%d" % (h, j))
+        for step in range(IH):
+            picked = keep.tile([P, IW], U32, name="tim_picked%d" % step, align_bytes=64)
+            nc.vector.tensor_copy(
+                picked[:], word_tab[1][:].bitcast(U32).indirect(tail_list[:, step * IW // 16 : (step + 1) * IW // 16])
+            )
+            for h, j, n, tag in banks:
+                if j <= step < j + n:
+                    cols = slice((step - j) * IW, (step - j + 1) * IW)
+                    mx_pass(accs[h, j][:, cols], h, 1, picked[:], step * IW, False, step == j + n - 1)
+        for step in range(IH):
+            for h, j, n, tag in banks:
+                if step == j + n - 1:
+                    for sh, sj, sn in stores:
+                        if sh == h and sj <= j < sj + sn:
+                            empty[h](results[h, sj][:, (j - sj) * IW : (j - sj + n) * IW], accs[h, j][:])
+            for h, j, n in stores:
+                if step == j + n - 1:
+                    nc.sync.dma_start(out=out[halves[h], j * IW : (j + n) * IW], in_=results[h, j][:])

@@ -218,8 +218,7 @@ def tile_attend_complexscores_kernel(
             (0, 2, 1, "z_fwd00"),
             (0, 3, 1, "z_fwd01"),
             (1, 0, 2, "z_fwd10"),
-            (1, 2, 1, "z_fwd11"),
-            (1, 3, 1, "z_back0"),
+            (1, 2, 2, "z_fwd11"),
         ]
         stores = [(0, 0, 1), (0, 1, 1), (1, 0, 2), (0, 2, 2), (1, 2, 2)]
         empty = (nc.scalar.copy, nc.vector.tensor_copy)

@@ -82,54 +82,64 @@ def tile_attend_complexscores_kernel(
             nc.sync.dma_start(out=word_tab[c][:], in_=src[0].rearrange("p n t -> p (n t)").bitcast(I32))
 
         halves = [slice(h * P, (h + 1) * P) for h in range(QH)]
-        rel = [keep.tile([P, 2, Q], F32, name="rel%d" % t) for t in range(PACK)]
+        whole = slice(0, Q)
+        rel = [keep.tile([P, 2, 2, Q], F32, name="rel%d" % u) for u in range(2)]
 
         def scalar_gather(dst, window):
             nc.scalar.activation(dst, window, COPY)
 
-        def gather_rel(c, first, n):
-            scalar_gather(rel[first][:, c, :], rel_tab[c, first].indirect(rel_list[:]))
-            for t in range(first + 1, first + n):
-                nc.vector.tensor_copy(rel[t][:, c, :], rel_tab[c, t].indirect(rel_list[:]))
+        def gather_rel(c):
+            scalar_gather(rel[0][:, c, 0, :], rel_tab[c, 0].indirect(rel_list[:]))
+            for t in range(1, PACK):
+                nc.vector.tensor_copy(rel[t // 2][:, c, t % 2, :], rel_tab[c, t].indirect(rel_list[:]))
 
         prod = {}
-        for c in range(2):
+        for b in range(2):
             for u in range(2):
-                prod[c, u] = keep.tile([P, 2, 2, Q], F32, name="prod%d%d" % (c, u))
+                prod[b, u] = keep.tile([P, 2, 2, Q], F32, name="prod%d%d" % (b, u))
+        hre_picked = [keep.tile([P, 2, Q], F32, name="hre_picked%d" % u) for u in range(2)]
 
-        def multiply(c, t, gathers, engine):
-            width = Q // len(gathers)
-            for k, gather in enumerate(gathers):
-                cols = slice(k * width, (k + 1) * width)
-                head = keep.tile([P, 1, width], F32, name="head%d%d%d" % (c, t, k))
-                gather(head[:, 0, :], head_tab[c, t].indirect(head_list[:, cols.start // 16 : cols.stop // 16]))
-                engine.tensor_tensor(
-                    prod[c, t // 2][:, t % 2, :, cols], head[:].to_broadcast([P, 2, width]), rel[t][:, :, cols], MULT
-                )
+        def gather_hre(t, gather):
+            gather(hre_picked[t // 2][:, t % 2, :], head_tab[0, t].indirect(head_list[:]))
 
-        x_pairs = [keep.tile([P, 2, P], F32, name="x_pairs%d" % h, align_bytes=64) for h in range(QH)]
+        def hre_times_rre(t):
+            u, e = divmod(t, 2)
+            nc.vector.tensor_tensor(prod[0, u][:, 0, e, :], hre_picked[u][:, e, :], rel[u][:, 0, e, :], MULT)
+
+        def hre_times_rim(u):
+            nc.vector.tensor_tensor(prod[0, u][:, 1], hre_picked[u][:], rel[u][:, 1], MULT)
+
+        def him_products(t, cols):
+            u, e = divmod(t, 2)
+            width = cols.stop - cols.start
+            name = "him_picked%d_%d" % (t, cols.start)
+            picked = keep.tile([P, 1, width], F32, name=name, tag=name, align_bytes=64)
+            scalar_gather(picked[:, 0, :], head_tab[1, t].indirect(head_list[:, cols.start // 16 : cols.stop // 16]))
+            nc.vector.tensor_tensor(
+                prod[1, u][:, :, e, cols], picked[:].to_broadcast([P, 2, width]), rel[u][:, :, e, cols], MULT
+            )
+
         z_back = [psum.tile([P, 2, P], F32, name="z_back%d" % h, tag="z_back%d" % h) for h in range(QH)]
 
-        def subtract_x(u):
-            for h in range(QH):
-                nc.vector.tensor_tensor(
-                    x_pairs[h][:, u, :].bitcast(BF16).rearrange("p (q e) -> p q e", e=2),
-                    prod[0, u][:, :, 0, halves[h]].rearrange("p e q -> p q e"),
-                    prod[1, u][:, :, 1, halves[h]].rearrange("p e q -> p q e"),
-                    SUB,
-                )
+        def subtract_x(x_pairs, u, cols):
+            nc.vector.tensor_tensor(
+                x_pairs[:, u, cols].bitcast(BF16).rearrange("p (q e) -> p q e", e=2),
+                prod[0, u][:, 0, :, cols].rearrange("p e q -> p q e"),
+                prod[1, u][:, 1, :, cols].rearrange("p e q -> p q e"),
+                SUB,
+            )
 
         def add_z(u):
             fwd = [psum.tile([P, 2, P], F32, name="z_fwd%d%d" % (u, h), tag="z_fwd%d%d" % (u, h)) for h in range(QH)]
-            for c in range(2):
+            for b in range(2):
                 for e in range(2):
                     for h in range(QH):
                         nc.tensor.matmul(
                             fwd[h][:, e, :],
-                            prod[c, u][:, e, 1 - c, halves[h]],
+                            prod[b, u][:, 1 - b, e, halves[h]],
                             ident[:],
-                            start=(c, e) == (0, 0),
-                            stop=(c, e) == (1, 1),
+                            start=(b, e) == (0, 0),
+                            stop=(b, e) == (1, 1),
                             is_transpose=True,
                         )
             return fwd
@@ -141,42 +151,45 @@ def tile_attend_complexscores_kernel(
                     z_back[h][:, u, :], turned[h].rearrange("q p e -> q (p e)").bitcast(F32), ident[:]
                 )
 
-        load_rel(0, 0, 4)
+        load_rel(0, 0, PACK)
         nc.sync.dma_start(rel_list[:], offs2)
-        load_rel(1, 0, 2)
         nc.sync.dma_start(tail_list[:], offs3)
         load_scales(0)
-        nc.sync.dma_start(head_list[:], offs)
-        load_head(0, 0, 2)
         load_scales(1)
+        nc.sync.dma_start(head_list[:], offs)
+        load_head(0, 0, PACK)
+        load_rel(1, 0, PACK)
         load_head(1, 0, 2)
-        load_rel(1, 2, 2)
-        load_head(0, 2, 2)
-        gather_rel(0, 0, 4)
-        gather_rel(1, 0, 2)
-        pick_scales(0)
-        pick_scales(1)
-        for c in range(2):
-            for t in range(2):
-                multiply(c, t, [scalar_gather], nc.vector)
-        subtract_x(0)
-        first_sums = add_z(0)
-        gather_rel(1, 2, 2)
-        for r in range(3):
-            place_scales(r)
         load_head(1, 2, 1)
         load_head(1, 3, 1)
+        gather_rel(0)
+        pick_scales(0)
+        pick_scales(1)
+        for r in range(3):
+            place_scales(r)
         load_words(0)
         place_scales(3)
         load_words(1)
-        multiply(0, 2, [scalar_gather], nc.vector)
-        multiply(0, 3, [nc.vector.tensor_copy], nc.vector)
-        multiply(1, 2, [scalar_gather], nc.vector)
-        multiply(1, 3, [nc.vector.tensor_copy, scalar_gather], nc.vector)
+        gather_hre(3, nc.vector.tensor_copy)
+        for t in range(3):
+            gather_hre(t, scalar_gather)
+        for t in (0, 3, 1, 2):
+            hre_times_rre(t)
+        gather_rel(1)
+        for u in range(2):
+            hre_times_rim(u)
+        for t in range(3):
+            him_products(t, whole)
+        for h in range(QH):
+            him_products(3, halves[h])
+        first_sums = add_z(0)
         first_turned = keep.tile([P, QH, P, 2], BF16, name="first_turned", tag="head_tab13")
         turn_back(0, first_sums, [first_turned[:, h] for h in range(QH)])
         second_sums = add_z(1)
-        subtract_x(1)
+        x_pairs = keep.tile([P, 2, Q], F32, name="x_pairs", tag="him_picked3_0", align_bytes=64)
+        subtract_x(x_pairs, 0, whole)
+        for h in range(QH):
+            subtract_x(x_pairs, 1, halves[h])
         turn_back(1, second_sums, [keep.tile([P, P, 2], BF16, name="turned%d" % h)[:] for h in range(QH)])
 
         grouped = keep.tile([P, 2, Q * PACK], BF16, name="grouped", tag="picked_scales", align_bytes=64)
@@ -196,7 +209,7 @@ def tile_attend_complexscores_kernel(
         tre_picked = keep.tile([P, I], U32, name="tre_picked", align_bytes=64)
         nc.vector.tensor_copy(tre_picked[:], word_tab[0][:].bitcast(U32).indirect(tail_list[:]))
         for h in range(QH):
-            quantise(0, h * P, P, x_pairs[h][:])
+            quantise(0, h * P, P, x_pairs[:, :, halves[h]])
         for h in range(QH):
             quantise(1, h * P, P, z_back[h][:])
 

@@ -22,6 +22,7 @@ PACK = 4
 QH = Q // P
 IH = 4
 IW = I // IH
+LINE = 4
 
 
 def tile_attend_complexscores_kernel(
@@ -65,7 +66,7 @@ def tile_attend_complexscores_kernel(
 
         def load_scales(c):
             src = (tre_scales, tim_scales)[c]
-            nc.sync.dma_start(out=scale_tab[c][32:96:4, :].bitcast(I32), in_=src[0].bitcast(I32))
+            nc.sync.dma_start(out=scale_tab[c][4:P:8, :].bitcast(I32), in_=src[0].bitcast(I32))
 
         picked_scales = keep.tile([P, 2 * I], U8, name="picked_scales", tag="picked_scales", align_bytes=64)
 
@@ -74,7 +75,7 @@ def tile_attend_complexscores_kernel(
 
         def place_scales(r):
             nc.sync.dma_start(
-                out=tail_scales[r:P:32, :].bitcast(I32), in_=picked_scales[32 + 4 * r : 96 : 16, :].bitcast(I32)
+                out=tail_scales[r:P:32, :].bitcast(I32), in_=picked_scales[4 + 8 * r : P : 32, :].bitcast(I32)
             )
 
         def load_words(c):
@@ -88,9 +89,14 @@ def tile_attend_complexscores_kernel(
         def scalar_gather(dst, window):
             nc.scalar.activation(dst, window, COPY)
 
-        def gather_rel(c):
-            scalar_gather(rel[0][:, c, 0, :], rel_tab[c, 0].indirect(rel_list[:]))
-            for t in range(1, PACK):
+        def gather_rel(c, on_scalar):
+            for t in range(1, on_scalar):
+                plane = keep.tile([P, U], F32, name="rel_plane%d%d" % (c, t))
+                nc.scalar.activation(plane[:], rel_tab[c, t], COPY)
+                rel_tab[c, t] = plane[:]
+            for t in range(on_scalar):
+                scalar_gather(rel[t // 2][:, c, t % 2, :], rel_tab[c, t].indirect(rel_list[:]))
+            for t in range(on_scalar, PACK):
                 nc.vector.tensor_copy(rel[t // 2][:, c, t % 2, :], rel_tab[c, t].indirect(rel_list[:]))
 
         prod = {}
@@ -123,9 +129,9 @@ def tile_attend_complexscores_kernel(
 
         def subtract_x(x_pairs, u, cols):
             nc.vector.tensor_tensor(
-                x_pairs[:, u, cols].bitcast(BF16).rearrange("p (q e) -> p q e", e=2),
-                prod[0, u][:, 0, :, cols].rearrange("p e q -> p q e"),
-                prod[1, u][:, 1, :, cols].rearrange("p e q -> p q e"),
+                x_pairs[:, u, cols].bitcast(BF16).rearrange("p (g i e) -> p g e i", e=2, i=LINE),
+                prod[0, u][:, 0, :, cols].rearrange("p e (g i) -> p g e i", i=LINE),
+                prod[1, u][:, 1, :, cols].rearrange("p e (g i) -> p g e i", i=LINE),
                 SUB,
             )
 
@@ -162,7 +168,7 @@ def tile_attend_complexscores_kernel(
         load_head(1, 0, 2)
         load_head(1, 2, 1)
         load_head(1, 3, 1)
-        gather_rel(0)
+        gather_rel(0, 1)
         pick_scales(0)
         pick_scales(1)
         for r in range(3):
@@ -175,19 +181,22 @@ def tile_attend_complexscores_kernel(
             gather_hre(t, scalar_gather)
         for t in (0, 3, 1, 2):
             hre_times_rre(t)
-        gather_rel(1)
-        for u in range(2):
+        gather_rel(1, 2)
+        for u in (1, 0):
             hre_times_rim(u)
-        for t in range(3):
-            him_products(t, whole)
+        x_pairs = keep.tile([P, 2, Q], F32, name="x_pairs", align_bytes=64)
+        for t in range(2):
+            for h in range(QH):
+                him_products(t, halves[h])
+        for h in range(QH):
+            subtract_x(x_pairs, 0, halves[h])
+        him_products(2, whole)
         for h in range(QH):
             him_products(3, halves[h])
         first_sums = add_z(0)
         first_turned = keep.tile([P, QH, P, 2], BF16, name="first_turned", tag="head_tab13")
         turn_back(0, first_sums, [first_turned[:, h] for h in range(QH)])
         second_sums = add_z(1)
-        x_pairs = keep.tile([P, 2, Q], F32, name="x_pairs", tag="him_picked3_0", align_bytes=64)
-        subtract_x(x_pairs, 0, whole)
         for h in range(QH):
             subtract_x(x_pairs, 1, halves[h])
         turn_back(1, second_sums, [keep.tile([P, P, 2], BF16, name="turned%d" % h)[:] for h in range(QH)])
@@ -226,17 +235,16 @@ def tile_attend_complexscores_kernel(
             )
 
         banks = [
-            (0, 0, 1, "acc0"),
-            (0, 1, 1, "acc1"),
-            (0, 2, 1, "z_fwd00"),
-            (0, 3, 1, "z_fwd01"),
-            (1, 0, 2, "z_fwd10"),
-            (1, 2, 2, "z_fwd11"),
+            (0, 0, 1, "acc0", nc.scalar.copy),
+            (0, 1, 1, "acc1", nc.scalar.copy),
+            (1, 0, 2, "z_fwd10", nc.scalar.copy),
+            (0, 2, 1, "z_fwd00", nc.vector.tensor_copy),
+            (0, 3, 1, "z_fwd01", nc.scalar.copy),
+            (1, 2, 2, "z_fwd11", nc.vector.tensor_copy),
         ]
         stores = [(0, 0, 1), (0, 1, 1), (1, 0, 2), (0, 2, 2), (1, 2, 2)]
-        empty = (nc.scalar.copy, nc.vector.tensor_copy)
         accs = {}
-        for h, j, n, tag in banks:
+        for h, j, n, tag, empty in sorted(banks, key=lambda bank: bank[:2]):
             accs[h, j] = psum.tile([P, n * IW], F32, name="acc%d%d" % (h, j), tag=tag)
             mx_pass(accs[h, j][:], h, 0, tre_picked[:, j * IW : (j + n) * IW], j * IW, True, False)
         results = {}
@@ -247,16 +255,16 @@ def tile_attend_complexscores_kernel(
             nc.vector.tensor_copy(
                 picked[:], word_tab[1][:].bitcast(U32).indirect(tail_list[:, step * IW // 16 : (step + 1) * IW // 16])
             )
-            for h, j, n, tag in banks:
+            for h, j, n, tag, empty in banks:
                 if j <= step < j + n:
                     cols = slice((step - j) * IW, (step - j + 1) * IW)
                     mx_pass(accs[h, j][:, cols], h, 1, picked[:], step * IW, False, step == j + n - 1)
         for step in range(IH):
-            for h, j, n, tag in banks:
+            for h, j, n, tag, empty in banks:
                 if step == j + n - 1:
                     for sh, sj, sn in stores:
                         if sh == h and sj <= j < sj + sn:
-                            empty[h](results[h, sj][:, (j - sj) * IW : (j - sj + n) * IW], accs[h, j][:])
+                            empty(results[h, sj][:, (j - sj) * IW : (j - sj + n) * IW], accs[h, j][:])
             for h, j, n in stores:
                 if step == j + n - 1:
                     nc.sync.dma_start(out=out[halves[h], j * IW : (j + n) * IW], in_=results[h, j][:])

@@ -22,7 +22,6 @@ PACK = 4
 QH = Q // P
 IH = 4
 IW = I // IH
-LINE = 4
 
 
 def tile_attend_complexscores_kernel(
@@ -31,6 +30,7 @@ def tile_attend_complexscores_kernel(
     nc = tc.nc
     with ExitStack() as ctx:
         keep = ctx.enter_context(tc.tile_pool(name="keep", bufs=1))
+        spare = ctx.enter_context(tc.tile_pool(name="spare", bufs=1))
         psum = ctx.enter_context(tc.psum_pool(name="psum", bufs=1))
 
         head_list = keep.tile([P, Q // 16], U16, name="head_list")
@@ -66,7 +66,7 @@ def tile_attend_complexscores_kernel(
 
         def load_scales(c):
             src = (tre_scales, tim_scales)[c]
-            nc.sync.dma_start(out=scale_tab[c][4:P:8, :].bitcast(I32), in_=src[0].bitcast(I32))
+            nc.sync.dma_start(out=scale_tab[c][32:96:4, :].bitcast(I32), in_=src[0].bitcast(I32))
 
         picked_scales = keep.tile([P, 2 * I], U8, name="picked_scales", tag="picked_scales", align_bytes=64)
 
@@ -75,7 +75,7 @@ def tile_attend_complexscores_kernel(
 
         def place_scales(r):
             nc.sync.dma_start(
-                out=tail_scales[r:P:32, :].bitcast(I32), in_=picked_scales[4 + 8 * r : P : 32, :].bitcast(I32)
+                out=tail_scales[r:P:32, :].bitcast(I32), in_=picked_scales[32 + 4 * r : 96 : 16, :].bitcast(I32)
             )
 
         def load_words(c):
@@ -91,7 +91,7 @@ def tile_attend_complexscores_kernel(
 
         def gather_rel(c, on_scalar):
             for t in range(1, on_scalar):
-                plane = keep.tile([P, U], F32, name="rel_plane%d%d" % (c, t))
+                plane = spare.tile([P, U], F32, name="rel_plane%d%d" % (c, t))
                 nc.scalar.activation(plane[:], rel_tab[c, t], COPY)
                 rel_tab[c, t] = plane[:]
             for t in range(on_scalar):
@@ -103,17 +103,14 @@ def tile_attend_complexscores_kernel(
         for b in range(2):
             for u in range(2):
                 prod[b, u] = keep.tile([P, 2, 2, Q], F32, name="prod%d%d" % (b, u))
+        x_pairs = [keep.tile([P, 2, P], F32, name="x_pairs%d" % h, align_bytes=64) for h in range(QH)]
         hre_picked = [keep.tile([P, 2, Q], F32, name="hre_picked%d" % u) for u in range(2)]
 
         def gather_hre(t, gather):
             gather(hre_picked[t // 2][:, t % 2, :], head_tab[0, t].indirect(head_list[:]))
 
-        def hre_times_rre(t):
-            u, e = divmod(t, 2)
-            nc.vector.tensor_tensor(prod[0, u][:, 0, e, :], hre_picked[u][:, e, :], rel[u][:, 0, e, :], MULT)
-
-        def hre_times_rim(u):
-            nc.vector.tensor_tensor(prod[0, u][:, 1], hre_picked[u][:], rel[u][:, 1], MULT)
+        def hre_products(c, u):
+            nc.vector.tensor_tensor(prod[0, u][:, c], hre_picked[u][:], rel[u][:, c], MULT)
 
         def him_products(t, cols):
             u, e = divmod(t, 2)
@@ -127,13 +124,14 @@ def tile_attend_complexscores_kernel(
 
         z_back = [psum.tile([P, 2, P], F32, name="z_back%d" % h, tag="z_back%d" % h) for h in range(QH)]
 
-        def subtract_x(x_pairs, u, cols):
-            nc.vector.tensor_tensor(
-                x_pairs[:, u, cols].bitcast(BF16).rearrange("p (g i e) -> p g e i", e=2, i=LINE),
-                prod[0, u][:, 0, :, cols].rearrange("p e (g i) -> p g e i", i=LINE),
-                prod[1, u][:, 1, :, cols].rearrange("p e (g i) -> p g e i", i=LINE),
-                SUB,
-            )
+        def subtract_x(u):
+            for h in range(QH):
+                nc.vector.tensor_tensor(
+                    x_pairs[h][:, u, :].bitcast(BF16).rearrange("p (q e) -> p q e", e=2),
+                    prod[0, u][:, 0, :, halves[h]].rearrange("p e q -> p q e"),
+                    prod[1, u][:, 1, :, halves[h]].rearrange("p e q -> p q e"),
+                    SUB,
+                )
 
         def add_z(u):
             fwd = [psum.tile([P, 2, P], F32, name="z_fwd%d%d" % (u, h), tag="z_fwd%d%d" % (u, h)) for h in range(QH)]
@@ -176,20 +174,19 @@ def tile_attend_complexscores_kernel(
         load_words(0)
         place_scales(3)
         load_words(1)
-        gather_hre(3, nc.vector.tensor_copy)
-        for t in range(3):
+        for t in (2, 3):
+            gather_hre(t, nc.vector.tensor_copy)
+        for t in (0, 1):
             gather_hre(t, scalar_gather)
-        for t in (0, 3, 1, 2):
-            hre_times_rre(t)
+        for u in (1, 0):
+            hre_products(0, u)
         gather_rel(1, 2)
         for u in (1, 0):
-            hre_times_rim(u)
-        x_pairs = keep.tile([P, 2, Q], F32, name="x_pairs", align_bytes=64)
+            hre_products(1, u)
         for t in range(2):
             for h in range(QH):
                 him_products(t, halves[h])
-        for h in range(QH):
-            subtract_x(x_pairs, 0, halves[h])
+        subtract_x(0)
         him_products(2, whole)
         for h in range(QH):
             him_products(3, halves[h])
@@ -197,8 +194,7 @@ def tile_attend_complexscores_kernel(
         first_turned = keep.tile([P, QH, P, 2], BF16, name="first_turned", tag="head_tab13")
         turn_back(0, first_sums, [first_turned[:, h] for h in range(QH)])
         second_sums = add_z(1)
-        for h in range(QH):
-            subtract_x(x_pairs, 1, halves[h])
+        subtract_x(1)
         turn_back(1, second_sums, [keep.tile([P, P, 2], BF16, name="turned%d" % h)[:] for h in range(QH)])
 
         grouped = keep.tile([P, 2, Q * PACK], BF16, name="grouped", tag="picked_scales", align_bytes=64)
@@ -218,7 +214,7 @@ def tile_attend_complexscores_kernel(
         tre_picked = keep.tile([P, I], U32, name="tre_picked", align_bytes=64)
         nc.vector.tensor_copy(tre_picked[:], word_tab[0][:].bitcast(U32).indirect(tail_list[:]))
         for h in range(QH):
-            quantise(0, h * P, P, x_pairs[:, :, halves[h]])
+            quantise(0, h * P, P, x_pairs[h][:])
         for h in range(QH):
             quantise(1, h * P, P, z_back[h][:])
 
@@ -235,16 +231,17 @@ def tile_attend_complexscores_kernel(
             )
 
         banks = [
-            (0, 0, 1, "acc0", nc.scalar.copy),
-            (0, 1, 1, "acc1", nc.scalar.copy),
-            (1, 0, 2, "z_fwd10", nc.scalar.copy),
-            (0, 2, 1, "z_fwd00", nc.vector.tensor_copy),
-            (0, 3, 1, "z_fwd01", nc.scalar.copy),
-            (1, 2, 2, "z_fwd11", nc.vector.tensor_copy),
+            (0, 0, 1, "acc0"),
+            (0, 1, 1, "acc1"),
+            (0, 2, 1, "z_fwd00"),
+            (0, 3, 1, "z_fwd01"),
+            (1, 0, 2, "z_fwd10"),
+            (1, 2, 2, "z_fwd11"),
         ]
         stores = [(0, 0, 1), (0, 1, 1), (1, 0, 2), (0, 2, 2), (1, 2, 2)]
+        empty = (nc.scalar.copy, nc.vector.tensor_copy)
         accs = {}
-        for h, j, n, tag, empty in sorted(banks, key=lambda bank: bank[:2]):
+        for h, j, n, tag in banks:
             accs[h, j] = psum.tile([P, n * IW], F32, name="acc%d%d" % (h, j), tag=tag)
             mx_pass(accs[h, j][:], h, 0, tre_picked[:, j * IW : (j + n) * IW], j * IW, True, False)
         results = {}
@@ -255,16 +252,16 @@ def tile_attend_complexscores_kernel(
             nc.vector.tensor_copy(
                 picked[:], word_tab[1][:].bitcast(U32).indirect(tail_list[:, step * IW // 16 : (step + 1) * IW // 16])
             )
-            for h, j, n, tag, empty in banks:
+            for h, j, n, tag in banks:
                 if j <= step < j + n:
                     cols = slice((step - j) * IW, (step - j + 1) * IW)
                     mx_pass(accs[h, j][:, cols], h, 1, picked[:], step * IW, False, step == j + n - 1)
         for step in range(IH):
-            for h, j, n, tag, empty in banks:
+            for h, j, n, tag in banks:
                 if step == j + n - 1:
                     for sh, sj, sn in stores:
                         if sh == h and sj <= j < sj + sn:
-                            empty(results[h, sj][:, (j - sj) * IW : (j - sj + n) * IW], accs[h, j][:])
+                            empty[h](results[h, sj][:, (j - sj) * IW : (j - sj + n) * IW], accs[h, j][:])
             for h, j, n in stores:
                 if step == j + n - 1:
                     nc.sync.dma_start(out=out[halves[h], j * IW : (j + n) * IW], in_=results[h, j][:])

@@ -73,9 +73,9 @@ def tile_attend_complexscores_kernel(
         def pick_scales(c):
             nc.vector.tensor_copy(picked_scales[:, c * I : (c + 1) * I], scale_tab[c][:].indirect(tail_list[:]))
 
-        def place_scales(r):
+        def place_scales(r, cols):
             nc.sync.dma_start(
-                out=tail_scales[r:P:32, :].bitcast(I32), in_=picked_scales[32 + 4 * r : 96 : 16, :].bitcast(I32)
+                out=tail_scales[r:P:32, cols].bitcast(I32), in_=picked_scales[32 + 4 * r : 96 : 16, cols].bitcast(I32)
             )
 
         def load_words(c):
@@ -170,9 +170,10 @@ def tile_attend_complexscores_kernel(
         pick_scales(0)
         pick_scales(1)
         for r in range(3):
-            place_scales(r)
+            place_scales(r, slice(0, 2 * I))
+        place_scales(3, slice(0, I))
         load_words(0)
-        place_scales(3)
+        place_scales(3, slice(I, 2 * I))
         load_words(1)
         for t in (2, 3):
             gather_hre(t, nc.vector.tensor_copy)
@@ -235,8 +236,9 @@ def tile_attend_complexscores_kernel(
             (0, 1, 1, "acc1"),
             (0, 2, 1, "z_fwd00"),
             (0, 3, 1, "z_fwd01"),
-            (1, 0, 2, "z_fwd10"),
-            (1, 2, 2, "z_fwd11"),
+            (1, 0, 1, "z_fwd10"),
+            (1, 1, 1, "z_fwd11"),
+            (1, 2, 2, "z_back0"),
         ]
         stores = [(0, 0, 1), (0, 1, 1), (1, 0, 2), (0, 2, 2), (1, 2, 2)]
         empty = (nc.scalar.copy, nc.vector.tensor_copy)
@@ -246,7 +248,7 @@ def tile_attend_complexscores_kernel(
             mx_pass(accs[h, j][:], h, 0, tre_picked[:, j * IW : (j + n) * IW], j * IW, True, False)
         results = {}
         for h, j, n in stores:
-            results[h, j] = keep.tile([P, n * IW], F32, name="result%d%d" % (h, j))
+            results[h, j] = keep.tile([P, n * IW], F32, name="result%d%d" % (h, j), align_bytes=256)
         for step in range(IH):
             picked = keep.tile([P, IW], U32, name="tim_picked%d" % step, align_bytes=64)
             nc.vector.tensor_copy(
@@ -261,7 +263,7 @@ def tile_attend_complexscores_kernel(
                 if step == j + n - 1:
                     for sh, sj, sn in stores:
                         if sh == h and sj <= j < sj + sn:
-                            empty[h](results[h, sj][:, (j - sj) * IW : (j - sj + n) * IW], accs[h, j][:])
+                            empty[h if step else 0](results[h, sj][:, (j - sj) * IW : (j - sj + n) * IW], accs[h, j][:])
             for h, j, n in stores:
                 if step == j + n - 1:
                     nc.sync.dma_start(out=out[halves[h], j * IW : (j + n) * IW], in_=results[h, j][:])

@@ -231,39 +231,29 @@ def tile_attend_complexscores_kernel(
                 stop=stop,
             )
 
-        banks = [
-            (0, 0, 1, "acc0"),
-            (0, 1, 1, "acc1"),
-            (0, 2, 1, "z_fwd00"),
-            (0, 3, 1, "z_fwd01"),
-            (1, 0, 1, "z_fwd10"),
-            (1, 1, 1, "z_fwd11"),
-            (1, 2, 2, "z_back0"),
-        ]
-        stores = [(0, 0, 1), (0, 1, 1), (1, 0, 2), (0, 2, 2), (1, 2, 2)]
-        empty = (nc.scalar.copy, nc.vector.tensor_copy)
+        bank_tags = (("acc0", "acc1", "z_fwd00", "z_fwd01"), ("z_fwd10", "z_fwd11", "z_back0", "z_back1"))
         accs = {}
-        for h, j, n, tag in banks:
-            accs[h, j] = psum.tile([P, n * IW], F32, name="acc%d%d" % (h, j), tag=tag)
-            mx_pass(accs[h, j][:], h, 0, tre_picked[:, j * IW : (j + n) * IW], j * IW, True, False)
-        results = {}
-        for h, j, n in stores:
-            results[h, j] = keep.tile([P, n * IW], F32, name="result%d%d" % (h, j), align_bytes=256)
+        for h in range(QH):
+            for step in range(IH):
+                accs[h, step] = psum.tile([P, IW], F32, name="acc%d%d" % (h, step), tag=bank_tags[h][step])
+                mx_pass(accs[h, step][:], h, 0, tre_picked[:, step * IW : (step + 1) * IW], step * IW, True, False)
+        results = [keep.tile([P, I], F32, name="result%d" % h, align_bytes=256) for h in range(QH)]
         for step in range(IH):
             picked = keep.tile([P, IW], U32, name="tim_picked%d" % step, align_bytes=64)
             nc.vector.tensor_copy(
                 picked[:], word_tab[1][:].bitcast(U32).indirect(tail_list[:, step * IW // 16 : (step + 1) * IW // 16])
             )
-            for h, j, n, tag in banks:
-                if j <= step < j + n:
-                    cols = slice((step - j) * IW, (step - j + 1) * IW)
-                    mx_pass(accs[h, j][:, cols], h, 1, picked[:], step * IW, False, step == j + n - 1)
+            for h in (step % 2, 1 - step % 2):
+                mx_pass(accs[h, step][:], h, 1, picked[:], step * IW, False, True)
+
+        def store(h, first, end):
+            cols = slice(first * IW, end * IW)
+            nc.sync.dma_start(out=out[halves[h], cols], in_=results[h][:, cols])
+
         for step in range(IH):
-            for h, j, n, tag in banks:
-                if step == j + n - 1:
-                    for sh, sj, sn in stores:
-                        if sh == h and sj <= j < sj + sn:
-                            empty[h if step else 0](results[h, sj][:, (j - sj) * IW : (j - sj + n) * IW], accs[h, j][:])
-            for h, j, n in stores:
-                if step == j + n - 1:
-                    nc.sync.dma_start(out=out[halves[h], j * IW : (j + n) * IW], in_=results[h, j][:])
+            lead, trail = step % 2, 1 - step % 2
+            cols = slice(step * IW, (step + 1) * IW)
+            nc.scalar.copy(results[lead][:, cols], accs[lead, step][:])
+            store(lead, max(step - 1, 0), step + 1)
+            (nc.vector.tensor_copy if step else nc.scalar.copy)(results[trail][:, cols], accs[trail, step][:])
+        store(trail, IH - 1, IH)

@@ -253,7 +253,9 @@ def tile_attend_complexscores_kernel(
         for step in range(IH):
             lead, trail = step % 2, 1 - step % 2
             cols = slice(step * IW, (step + 1) * IW)
-            nc.scalar.copy(results[lead][:, cols], accs[lead, step][:])
-            store(lead, max(step - 1, 0), step + 1)
-            (nc.vector.tensor_copy if step else nc.scalar.copy)(results[trail][:, cols], accs[trail, step][:])
+            for h in (lead, trail):
+                copy = nc.vector.tensor_copy if h == 1 and step >= IH - 2 else nc.scalar.copy
+                copy(results[h][:, cols], accs[h, step][:])
+                if h == lead:
+                    store(lead, max(step - 1, 0), step + 1)
         store(trail, IH - 1, IH)

from contextlib import ExitStack

import concourse.mybir as mybir
from concourse.masks import make_identity

D, T, U, Q, V, I = 512, 1024, 512, 256, 2048, 512
FLOPS = 2 * 2 * D * Q * I

F32 = mybir.dt.float32
BF16 = mybir.dt.bfloat16
I32 = mybir.dt.int32
U32 = mybir.dt.uint32
U16 = mybir.dt.uint16
U8 = mybir.dt.uint8
FP8X4 = mybir.dt.float8_e4m3fn_x4
MULT = mybir.AluOpType.mult
SUB = mybir.AluOpType.subtract
COPY = mybir.ActivationFunctionType.Copy

P = 128
PACK = 4
QH = Q // P
IH = 4
IW = I // IH


def tile_attend_complexscores_kernel(
    tc, hre, him, rre, rim, tre_words, tre_scales, tim_words, tim_scales, offs, offs2, offs3, out
):
    nc = tc.nc
    with ExitStack() as ctx:
        keep = ctx.enter_context(tc.tile_pool(name="keep", bufs=1))
        spare = ctx.enter_context(tc.tile_pool(name="spare", bufs=1))
        psum = ctx.enter_context(tc.psum_pool(name="psum", bufs=1))

        head_list = keep.tile([P, Q // 16], U16, name="head_list")
        rel_list = keep.tile([P, Q // 16], U16, name="rel_list")
        tail_list = keep.tile([P, I // 16], U16, name="tail_list")

        scale_tab = [keep.tile([P, V], U8, name="scale_tab%d" % c) for c in range(2)]
        tail_scales = keep.tile([P, 2 * I], U8, name="tail_scales", align_bytes=64)
        nc.gpsimd.memset(scale_tab[0][:].bitcast(I32), 0)
        nc.vector.memset(scale_tab[1][:].bitcast(I32), 0)
        nc.vector.memset(tail_scales[:].bitcast(I32), 0)
        ident = keep.tile([P, P], F32, name="ident")
        make_identity(nc, ident[:])
        word_tab = [keep.tile([P, V], I32, name="word_tab%d" % c, align_bytes=64) for c in range(2)]

        rel_src = [src.rearrange("(p t) u -> p (t u)", t=PACK) for src in (rre, rim)]
        head_src = [src.rearrange("(p t) n -> p (t n)", t=PACK) for src in (hre, him)]
        rel_tab = {}
        head_tab = {}

        def load_rel(c, t, n):
            tab = keep.tile([P, n * U], F32, name="rel_tab%d%d" % (c, t))
            nc.sync.dma_start(out=tab[:], in_=rel_src[c][:, t * U : (t + n) * U])
            rel_tab[c, t] = tab[:]
            for e in range(1, n):
                rel_tab[c, t + e] = tab[:, e * U : (e + 1) * U]

        def load_head(c, t, n):
            tab = keep.tile([P, n * T], F32, name="head_tab%d%d" % (c, t), tag="head_tab%d%d" % (c, t))
            nc.sync.dma_start(out=tab[:], in_=head_src[c][:, t * T : (t + n) * T])
            for e in range(n):
                head_tab[c, t + e] = tab[:, e * T : (e + 1) * T]

        def load_scales(c):
            src = (tre_scales, tim_scales)[c]
            nc.sync.dma_start(out=scale_tab[c][32:96:4, :].bitcast(I32), in_=src[0].bitcast(I32))

        picked_scales = keep.tile([P, 2 * I], U8, name="picked_scales", tag="picked_scales", align_bytes=64)

        def pick_scales(c):
            nc.vector.tensor_copy(picked_scales[:, c * I : (c + 1) * I], scale_tab[c][:].indirect(tail_list[:]))

        def place_scales(r, cols):
            nc.sync.dma_start(
                out=tail_scales[r:P:32, cols].bitcast(I32), in_=picked_scales[32 + 4 * r : 96 : 16, cols].bitcast(I32)
            )

        def load_words(c):
            src = (tre_words, tim_words)[c]
            nc.sync.dma_start(out=word_tab[c][:], in_=src[0].rearrange("p n t -> p (n t)").bitcast(I32))

        halves = [slice(h * P, (h + 1) * P) for h in range(QH)]
        whole = slice(0, Q)
        rel = [keep.tile([P, 2, 2, Q], F32, name="rel%d" % u) for u in range(2)]

        def scalar_gather(dst, window):
            nc.scalar.activation(dst, window, COPY)

        def gather_rel(c, on_scalar):
            for t in range(1, on_scalar):
                plane = spare.tile([P, U], F32, name="rel_plane%d%d" % (c, t))
                nc.scalar.activation(plane[:], rel_tab[c, t], COPY)
                rel_tab[c, t] = plane[:]
            for t in range(on_scalar):
                scalar_gather(rel[t // 2][:, c, t % 2, :], rel_tab[c, t].indirect(rel_list[:]))
            for t in range(on_scalar, PACK):
                nc.vector.tensor_copy(rel[t // 2][:, c, t % 2, :], rel_tab[c, t].indirect(rel_list[:]))

        prod = {}
        for b in range(2):
            for u in range(2):
                prod[b, u] = keep.tile([P, 2, 2, Q], F32, name="prod%d%d" % (b, u))
        x_pairs = [keep.tile([P, 2, P], F32, name="x_pairs%d" % h, align_bytes=64) for h in range(QH)]
        hre_picked = [keep.tile([P, 2, Q], F32, name="hre_picked%d" % u) for u in range(2)]

        def gather_hre(t, gather):
            gather(hre_picked[t // 2][:, t % 2, :], head_tab[0, t].indirect(head_list[:]))

        def hre_products(c, u):
            nc.vector.tensor_tensor(prod[0, u][:, c], hre_picked[u][:], rel[u][:, c], MULT)

        def him_products(t, cols):
            u, e = divmod(t, 2)
            width = cols.stop - cols.start
            name = "him_picked%d_%d" % (t, cols.start)
            picked = keep.tile([P, 1, width], F32, name=name, tag=name, align_bytes=64)
            scalar_gather(picked[:, 0, :], head_tab[1, t].indirect(head_list[:, cols.start // 16 : cols.stop // 16]))
            nc.vector.tensor_tensor(
                prod[1, u][:, :, e, cols], picked[:].to_broadcast([P, 2, width]), rel[u][:, :, e, cols], MULT
            )

        z_back = [psum.tile([P, 2, P], F32, name="z_back%d" % h, tag="z_back%d" % h) for h in range(QH)]

        def subtract_x(u):
            for h in range(QH):
                nc.vector.tensor_tensor(
                    x_pairs[h][:, u, :].bitcast(BF16).rearrange("p (q e) -> p q e", e=2),
                    prod[0, u][:, 0, :, halves[h]].rearrange("p e q -> p q e"),
                    prod[1, u][:, 1, :, halves[h]].rearrange("p e q -> p q e"),
                    SUB,
                )

        def add_z(u):
            fwd = [psum.tile([P, 2, P], F32, name="z_fwd%d%d" % (u, h), tag="z_fwd%d%d" % (u, h)) for h in range(QH)]
            for b in range(2):
                for e in range(2):
                    for h in range(QH):
                        nc.tensor.matmul(
                            fwd[h][:, e, :],
                            prod[b, u][:, 1 - b, e, halves[h]],
                            ident[:],
                            start=(b, e) == (0, 0),
                            stop=(b, e) == (1, 1),
                            is_transpose=True,
                        )
            return fwd

        def turn_back(u, fwd, turned):
            for h in range(QH):
                nc.scalar.copy(turned[h], fwd[h][:].rearrange("q e p -> q p e"))
                nc.tensor.transpose(
                    z_back[h][:, u, :], turned[h].rearrange("q p e -> q (p e)").bitcast(F32), ident[:]
                )

        load_rel(0, 0, PACK)
        nc.sync.dma_start(rel_list[:], offs2)
        nc.sync.dma_start(tail_list[:], offs3)
        load_scales(0)
        load_scales(1)
        nc.sync.dma_start(head_list[:], offs)
        load_head(0, 0, PACK)
        load_rel(1, 0, PACK)
        load_head(1, 0, 2)
        load_head(1, 2, 1)
        load_head(1, 3, 1)
        gather_rel(0, 1)
        pick_scales(0)
        pick_scales(1)
        for r in range(3):
            place_scales(r, slice(0, 2 * I))
        place_scales(3, slice(0, I))
        load_words(0)
        place_scales(3, slice(I, 2 * I))
        load_words(1)
        for t in (2, 3):
            gather_hre(t, nc.vector.tensor_copy)
        for t in (0, 1):
            gather_hre(t, scalar_gather)
        for u in (1, 0):
            hre_products(0, u)
        gather_rel(1, 2)
        for u in (1, 0):
            hre_products(1, u)
        for t in range(2):
            for h in range(QH):
                him_products(t, halves[h])
        subtract_x(0)
        him_products(2, whole)
        for h in range(QH):
            him_products(3, halves[h])
        first_sums = add_z(0)
        first_turned = keep.tile([P, QH, P, 2], BF16, name="first_turned", tag="head_tab13")
        turn_back(0, first_sums, [first_turned[:, h] for h in range(QH)])
        second_sums = add_z(1)
        subtract_x(1)
        turn_back(1, second_sums, [keep.tile([P, P, 2], BF16, name="turned%d" % h)[:] for h in range(QH)])

        grouped = keep.tile([P, 2, Q * PACK], BF16, name="grouped", tag="picked_scales", align_bytes=64)
        codes = {}
        scales = {}

        def quantise(w, first, width, pairs):
            source = grouped[:, w, first * PACK : (first + width) * PACK]
            nc.scalar.copy(source.bitcast(F32).rearrange("p (q u) -> p q u", u=2), pairs.rearrange("p u q -> p q u"))
            cd = keep.tile([P, width], U32, name="codes%d%d" % (w, first), align_bytes=64)
            sc = keep.tile([P, width], U8, name="scales%d%d" % (w, first), align_bytes=64)
            nc.vector.quantize_mx(out=cd[:].bitcast(FP8X4), scales=sc[:], in_=source)
            for lo in range(0, width, P):
                codes[w, (first + lo) // P] = cd[:, lo : lo + P]
                scales[w, (first + lo) // P] = sc[:, lo : lo + P]

        tre_picked = keep.tile([P, I], U32, name="tre_picked", align_bytes=64)
        nc.vector.tensor_copy(tre_picked[:], word_tab[0][:].bitcast(U32).indirect(tail_list[:]))
        for h in range(QH):
            quantise(0, h * P, P, x_pairs[h][:])
        for h in range(QH):
            quantise(1, h * P, P, z_back[h][:])

        def mx_pass(acc, h, w, words, first, start, stop):
            width = acc.shape[-1]
            nc.tensor.matmul_mx(
                out=acc,
                lhsT=codes[w, h].bitcast(FP8X4),
                lhsT_scale=scales[w, h],
                rhs=words.bitcast(FP8X4),
                rhs_scale=tail_scales[:, w * I + first : w * I + first + width],
                start=start,
                stop=stop,
            )

        bank_tags = (("acc0", "acc1", "z_fwd00", "z_fwd01"), ("z_fwd10", "z_fwd11", "z_back0", "z_back1"))
        accs = {}
        for h in range(QH):
            for step in range(IH):
                accs[h, step] = psum.tile([P, IW], F32, name="acc%d%d" % (h, step), tag=bank_tags[h][step])
                mx_pass(accs[h, step][:], h, 0, tre_picked[:, step * IW : (step + 1) * IW], step * IW, True, False)
        results = [keep.tile([P, I], F32, name="result%d" % h, align_bytes=256) for h in range(QH)]
        for step in range(IH):
            picked = keep.tile([P, IW], U32, name="tim_picked%d" % step, align_bytes=64)
            nc.vector.tensor_copy(
                picked[:], word_tab[1][:].bitcast(U32).indirect(tail_list[:, step * IW // 16 : (step + 1) * IW // 16])
            )
            for h in (step % 2, 1 - step % 2):
                mx_pass(accs[h, step][:], h, 1, picked[:], step * IW, False, True)

        def store(h, first, end):
            cols = slice(first * IW, end * IW)
            nc.sync.dma_start(out=out[halves[h], cols], in_=results[h][:, cols])

        for step in range(IH):
            lead, trail = step % 2, 1 - step % 2
            cols = slice(step * IW, (step + 1) * IW)
            for h in (lead, trail):
                copy = nc.vector.tensor_copy if h == 1 and step >= IH - 2 else nc.scalar.copy
                copy(results[h][:, cols], accs[h, step][:])
                if h == lead:
                    store(lead, max(step - 1, 0), step + 1)
        store(trail, IH - 1, IH)
